import numpy as np
import ml_dtypes


def mxq(x, axis, fmt="e4m3"):
    dtype, down = {"e4m3": (ml_dtypes.float8_e4m3fn, 7), "e5m2": (ml_dtypes.float8_e5m2, 14)}[fmt]
    v = np.moveaxis(np.asarray(x, np.float32).astype(ml_dtypes.bfloat16).astype(np.float64), axis, -1)
    blocks = v.reshape(v.shape[:-1] + (-1, 32))
    amax = np.abs(blocks).max(-1, keepdims=True)
    byte = np.maximum(np.where(amax > 0, np.frexp(amax)[1] - 1 + 127, 0) - down, 1)
    scale = np.exp2(byte - 127.0)
    codes = (blocks / scale).astype(np.float32).astype(dtype).astype(np.float64)
    return np.moveaxis((codes * scale).reshape(v.shape), -1, axis)


WIDE = False


def mx_kscale(k):
    if not WIDE:
        return np.ones(k)
    levels = np.array([10, -10, 5, -5, 0])
    if k % 512:
        return np.exp2(np.random.permutation(np.resize(levels, k // 32))).repeat(32)
    a = np.empty((k // 512, 16))
    for p in range(k // 512):
        a[p, :8] = np.random.permutation(np.resize(levels, 8))
        for g in range(8):
            far = levels[np.abs(levels - a[p, g]) >= 10]
            a[p, g + 8] = far[np.random.randint(len(far))]
    return np.exp2(a.ravel()).repeat(32)


def f64(x):
    return np.asarray(x).astype(np.float64)


def striped(idx):
    return np.tile(idx.reshape(-1, 16).T, (8, 1)).astype(np.uint16)


def unstriped(offs):
    return offs[:16].T.reshape(-1).astype(np.int64)


def silu(v):
    return v / (1.0 + np.exp(-np.maximum(v, -700.0)))


K, T, E, C, H, N = 512, 512, 8, 128, 512, 128


def by_expert(wq, xq):
    return np.concatenate([wq[e].T @ xq[:, e * C:(e + 1) * C] for e in range(E)], axis=1)


def setup_inputs():
    n = np.random.standard_normal
    s = mx_kscale(K)[:, None]
    u = mx_kscale(H)
    first = np.random.permutation(np.repeat(np.arange(E), T // E))
    second = (first + 1 + np.random.permutation(np.repeat(np.arange(E - 1), -(-T // (E - 1)))[:T])) % E
    while np.bincount(second, minlength=E).max() != T // E:
        load = np.bincount(second, minlength=E); hi, lo = int(load.argmax()), int(load.argmin())
        t = np.flatnonzero((second == hi) & (first != lo))[0]; second[t] = lo
    slot_token = np.empty(E * C, np.int64); pos = np.empty((2, T), np.int64); fill = np.zeros(E, np.int64)
    place = np.stack([np.random.permutation(C) for _ in range(E)])
    for r, deal in enumerate((first, second)):
        for t in np.random.permutation(T):
            e = deal[t]; j = e * C + place[e, fill[e]]; fill[e] += 1; slot_token[j] = t; pos[r, t] = j
    g = np.random.uniform(0.2, 0.8, T)
    return {
        "xT": (n((K, T)) * s).astype(np.float32),
        "w1": (n((E, K, H)) / np.sqrt(K) / s[None]).astype(np.float32),
        "w3": (n((E, K, H)) / np.sqrt(K) / s[None] * u[None, None, :]).astype(np.float32),
        "w2": (n((E, H, N)) / np.sqrt(H) / u[None, :, None]).astype(np.float32),
        "gate": np.stack([np.tile(g, (N, 1)), np.tile(1.0 - g, (N, 1))]).astype(np.float32),
        "offs": striped(slot_token),
        "pos1": striped(pos[0]),
        "pos2": striped(pos[1]),
    }


def reference(xT, w1, w3, w2, gate, offs, pos1, pos2):
    idx = unstriped(offs)
    xq = mxq(f64(xT)[:, idx], 0, "e4m3")
    h = silu(by_expert(mxq(f64(w1), 1, "e4m3"), xq))
    h = h * by_expert(mxq(f64(w3), 1, "e4m3"), xq)
    y = by_expert(mxq(f64(w2), 1, "e4m3"), mxq(h, 0, "e4m3"))
    return f64(gate[0]) * y[:, unstriped(pos1)] + f64(gate[1]) * y[:, unstriped(pos2)]

@@ -1,0 +1,247 @@
+from contextlib import ExitStack
+
+import concourse.mybir as mybir
+
+K, T, E, C, H, N = 512, 512, 8, 128, 512, 128
+SLOTS = E * C
+FLOPS = 2 * SLOTS * (2 * K * H + H * N)
+
+F32 = mybir.dt.float32
+BF16 = mybir.dt.bfloat16
+U32 = mybir.dt.uint32
+U16 = mybir.dt.uint16
+U8 = mybir.dt.uint8
+FP8X4 = mybir.dt.float8_e4m3fn_x4
+MULT = mybir.AluOpType.mult
+ADD = mybir.AluOpType.add
+SILU = mybir.ActivationFunctionType.Silu
+
+P = 128
+J = 4
+LOADS = "offs xa xb w10 w30 w11 w31 pos w12 w32 w13 w33 w14 w34 w15 w35 w16 w36 w17 w37 w20 w24 w26 gate".split()
+GATHERS = ((0, 2), (2, 3), (5, 3))
+GATHER_AT = {0: 0, 1: 1, 3: 2}
+Y_GROUPS = ((0, 1, 2, 3), (4, 5), (6, 7))
+W2_GROUPS = ((0, 1, 2, 3), (4, 5), (6, 7))
+W2_AT = {8: ((0, 1, 2, 3), (4, 5), (6, 7))}
+W2_ON_VECTOR = (3, 5, 6, 7)
+V1 = {7: 64}
+S3 = {7: 48}
+SEPARATE = (7,)
+XV = (256, 256)
+
+
+def tile_routed_moe_kernel(tc, xT, w1, w3, w2, gate, offs, pos1, pos2, out):
+    nc = tc.nc
+    with ExitStack() as ctx:
+        held = ctx.enter_context(tc.tile_pool(name="held", bufs=1))
+        stage = ctx.enter_context(tc.tile_pool(name="stage", bufs=2))
+        psum = ctx.enter_context(tc.psum_pool(name="psum", bufs=3))
+
+        offs_t = held.tile([P, SLOTS // 16], U16, name="offs_t")
+        pos1_t = held.tile([P, T // 16], U16, name="pos1_t")
+        pos2_t = held.tile([P, T // 16], U16, name="pos2_t")
+        x_raw = [held.tile([P, J, T // 2], F32, name=f"x_raw{h}") for h in range(2)]
+        gates = held.tile([P, 2, T], F32, name="gates")
+        w1_raw = [held.tile([P, J * H], F32, name=f"w1_raw{e}") for e in range(E)]
+        w3_raw = [held.tile([P, J * H], F32, name=f"w3_raw{e}") for e in range(E)]
+        w2_raw = {g: held.tile([P, len(g), J * N], F32, name=f"w2_raw{g[0]}") for g in W2_GROUPS}
+
+        warm = held.tile([P, 1], F32, name="warm")
+        nc.vector.memset(warm[:], 0.0)
+        nc.scalar.activation(warm[:], warm[:], SILU)
+
+        for name in LOADS:
+            if name == "offs":
+                nc.sync.dma_start(offs_t[:], offs)
+            elif name == "pos":
+                nc.sync.dma_start(pos1_t[:], pos1)
+                nc.sync.dma_start(pos2_t[:], pos2)
+            elif name[0] == "x":
+                h = "ab".index(name[1])
+                nc.sync.dma_start(out=x_raw[h][:], in_=xT[:, h * (T // 2):(h + 1) * (T // 2)].rearrange("(p j) t -> p j t", j=J))
+            elif name == "gate":
+                nc.sync.dma_start(out=gates[:], in_=gate.rearrange("g p t -> p g t"))
+            elif name[:2] == "w2":
+                for g in W2_GROUPS:
+                    if g[0] == int(name[2]):
+                        nc.sync.dma_start(out=w2_raw[g][:], in_=w2[g[0]:g[-1] + 1, :, :].rearrange("e (p j) n -> p e (j n)", j=J))
+            else:
+                e = int(name[2])
+                raw, w = (w1_raw[e], w1) if name[1] == "1" else (w3_raw[e], w3)
+                nc.sync.dma_start(out=raw[:], in_=w[e, :, :].rearrange("(p j) h -> p (j h)", j=J))
+
+        x_codes = held.tile([P, T], U32, name="x_codes", align_bytes=64)
+        x_scales = held.tile([P, T], U8, name="x_scales", align_bytes=64)
+        nc.gpsimd.memset(x_scales[:], 0)
+        x_grouped = held.tile([P, T * J], BF16, name="x_grouped", align_bytes=64)
+        for h in range(2):
+            x_src = x_raw[h][:].rearrange("p j (c i) -> p c j i", i=4)
+            x_dst = x_grouped[:, h * 1024:(h + 1) * 1024].rearrange("p (c i j) -> p c j i", i=4, j=J)
+            cut = XV[h] // 4
+            if cut < 64:
+                nc.scalar.copy(out=x_dst[:, cut:64], in_=x_src[:, cut:64])
+            if cut:
+                nc.vector.tensor_copy(out=x_dst[:, 0:cut], in_=x_src[:, 0:cut])
+            half = slice(h * (T // 2), (h + 1) * (T // 2))
+            nc.vector.quantize_mx(out=x_codes[:, half].bitcast(FP8X4), scales=x_scales[:, half],
+                                  in_=x_grouped[:, h * 1024:(h + 1) * 1024])
+
+        s_codes = held.tile([P, SLOTS], U32, name="s_codes", align_bytes=64)
+        s_scales = held.tile([P, SLOTS], U8, name="s_scales", align_bytes=64)
+        y_sb = held.tile([P, SLOTS], F32, name="y_sb")
+        live = {}
+
+        def gather(first, count):
+            cols = slice(first * C, (first + count) * C)
+            lst = offs_t[:, first * C // 16:(first + count) * C // 16]
+            nc.vector.tensor_copy(s_codes[:, cols], x_codes[:].indirect(lst))
+            nc.vector.tensor_copy(s_scales[:, cols], x_scales[:].indirect(lst))
+
+        def up_views(raw, grouped, m0, m1):
+            src = raw[:].rearrange("p (j m t) -> p m j t", j=J, t=4)
+            dst = grouped.rearrange("p (t m j) -> p m j t", t=4, j=J)
+            return src[:, m0:m1], dst[:, m0:m1]
+
+        def inter(which, e):
+            if which == 0:
+                live["g", e] = stage.tile([P, 2, H * J], BF16, name="grouped", align_bytes=64)
+            raw = (w1_raw, w3_raw)[which][e]
+            v = V1.get(e, 0) if which == 0 else 128 - S3.get(e, 0)
+            parts = [(0, v, 128)]
+            for lo, cut, hi in parts:
+                if hi > cut:
+                    src, dst = up_views(raw, live["g", e][:, which, :], cut, hi)
+                    nc.scalar.copy(out=dst, in_=src)
+                if cut > lo:
+                    src, dst = up_views(raw, live["g", e][:, which, :], lo, cut)
+                    nc.vector.tensor_copy(out=dst, in_=src)
+
+        def products(which, e):
+            codes, scales = live["q", e]
+            acc = psum.tile([P, 4, C], F32, name=f"acc{which}", bufs=3)
+            cols = slice(e * C, (e + 1) * C)
+            for t in range(4):
+                blk = slice(which * H + t * P, which * H + (t + 1) * P)
+                nc.tensor.matmul_mx(
+                    out=acc[:, t, :], lhsT=codes[:, blk].bitcast(FP8X4), lhsT_scale=scales[:, blk],
+                    rhs=s_codes[:, cols].bitcast(FP8X4), rhs_scale=s_scales[:, cols], start=True, stop=True)
+            live["acc", which, e] = acc
+
+        def quant(whichs, e):
+            if whichs[0] == 0:
+                codes = stage.tile([P, 2 * H], U32, name="codes", align_bytes=64)
+                scales = stage.tile([P, 2 * H], U8, name="scales", align_bytes=64)
+                live["q", e] = codes, scales
+            codes, scales = live["q", e]
+            cols = slice(whichs[0] * H, (whichs[-1] + 1) * H)
+            words = slice(whichs[0] * H * J, (whichs[-1] + 1) * H * J)
+            nc.vector.quantize_mx(out=codes[:, cols].bitcast(FP8X4), scales=scales[:, cols],
+                                  in_=live["g", e][:].rearrange("p w k -> p (w k)")[:, words])
+            for which in whichs:
+                products(which, e)
+
+        def silu(e):
+            if e == E - 1:
+                sil = held.tile([P, C, 4], F32, name="sil_last", tag="last", align_bytes=64)
+            else:
+                sil = stage.tile([P, C, 4], F32, name="sil")
+            nc.scalar.activation(sil[:], live["acc", 0, e][:].rearrange("p t c -> p c t"), SILU)
+            live["sil", e] = sil
+
+        def inter2(g):
+            tag = "last" if g[-1] == E - 1 else f"grp2_{g[0]}"
+            grouped = held.tile([P, len(g), N * J], BF16, name=f"grp2_{g[0]}", tag=tag, align_bytes=64)
+            src = w2_raw[g][:].rearrange("p e (j c i) -> p e c j i", j=J, i=4)
+            dst = grouped[:].rearrange("p e (c i j) -> p e c j i", i=4, j=J)
+            on_vector = [e for e in g if e in W2_ON_VECTOR]
+            cut = on_vector[0] - g[0] if on_vector else len(g)
+            if cut:
+                nc.scalar.copy(out=dst[:, 0:cut], in_=src[:, 0:cut])
+            if cut < len(g):
+                nc.vector.tensor_copy(out=dst[:, cut:], in_=src[:, cut:])
+            codes = held.tile([P, len(g), N], U32, name=f"cod2_{g[0]}", align_bytes=64)
+            scales = held.tile([P, len(g), N], U8, name=f"scl2_{g[0]}", align_bytes=64)
+            nc.vector.quantize_mx(
+                out=codes[:].rearrange("p e n -> p (e n)").bitcast(FP8X4),
+                scales=scales[:].rearrange("p e n -> p (e n)"), in_=grouped[:].rearrange("p e n -> p (e n)"))
+            for i, e in enumerate(g):
+                live["w2", e] = codes[:, i, :], scales[:, i, :]
+
+        h_group_of = {e: g for g in ((0, 1), (2, 3), (4, 5), (6,), (7,)) for e in g}
+        group_of = {e: g for g in Y_GROUPS for e in g}
+
+        def hid(e):
+            grp = h_group_of[e]
+            if e == grp[0]:
+                live["hb", grp] = stage.tile([P, 2, C, 4], BF16, name="hb", align_bytes=64)
+            nc.vector.tensor_tensor(live["hb", grp][:, e - grp[0]], live["acc", 1, e][:].rearrange("p t c -> p c t"), live["sil", e][:], MULT)
+
+        def quanth(grp):
+            n = len(grp)
+            codes = stage.tile([P, 2, C], U32, name="codh", align_bytes=64, bufs=E)
+            scales = stage.tile([P, 2, C], U8, name="sclh", align_bytes=64, bufs=E)
+            nc.vector.quantize_mx(out=codes[:, 0:n].rearrange("p e c -> p (e c)").bitcast(FP8X4),
+                                  scales=scales[:, 0:n].rearrange("p e c -> p (e c)"),
+                                  in_=live["hb", grp][:, 0:n].rearrange("p e c t -> p (e c t)"))
+            for i, e in enumerate(grp):
+                live["qh", e] = codes[:, i, :], scales[:, i, :]
+
+        def down(e):
+            codes, scales = live["qh", e]
+            grp = group_of[e]
+            if e == grp[0]:
+                live["y", grp] = psum.tile([P, 4, C], F32, name="acc_y", bufs=2)
+            w2c, w2s = live["w2", e]
+            nc.tensor.matmul_mx(
+                out=live["y", grp][:, e - grp[0], :], lhsT=w2c.bitcast(FP8X4), lhsT_scale=w2s,
+                rhs=codes.bitcast(FP8X4), rhs_scale=scales, start=True, stop=True)
+
+        def fetch(grp):
+            nc.scalar.copy(
+                out=y_sb[:, grp[0] * C:(grp[-1] + 1) * C].rearrange("p (g c) -> p g c", c=C),
+                in_=live["y", grp][:, 0:len(grp), :])
+
+        pending = []
+        for e in range(E + 1):
+            if e in GATHER_AT:
+                gather(*GATHERS[GATHER_AT[e]])
+            if e < E:
+                inter(0, e)
+                if e in SEPARATE:
+                    quant((0,), e)
+                    silu(e)
+                    if e > 0:
+                        hid(e - 1)
+                inter(1, e)
+            if 0 < e < E and e not in SEPARATE:
+                hid(e - 1)
+            if e < E:
+                if e in SEPARATE:
+                    quant((1,), e)
+                else:
+                    quant((0, 1), e)
+                    silu(e)
+            if e == E:
+                hid(e - 1)
+            if e > 0:
+                if e - 1 == h_group_of[e - 1][-1]:
+                    quanth(h_group_of[e - 1])
+                    pending.extend(h_group_of[e - 1])
+            for g in W2_AT.get(e, ()):
+                inter2(g)
+            for d in list(pending):
+                if ("w2", d) in live:
+                    down(d)
+                    pending.remove(d)
+                    if d == group_of[d][-1]:
+                        fetch(group_of[d])
+
+        r1 = held.tile([P, T], F32, name="r1")
+        r2 = held.tile([P, T], F32, name="r2")
+        nc.vector.tensor_tensor(r1[:], y_sb[:].indirect(pos1_t[:]), gates[:, 0, :], MULT)
+        nc.vector.tensor_tensor(r2[:], y_sb[:].indirect(pos2_t[:]), gates[:, 1, :], MULT)
+        res = held.tile([P, T], F32, name="res")
+        for queue, toks in ((nc.sync, slice(0, T // 2)), (nc.scalar, slice(T // 2, T))):
+            nc.vector.tensor_tensor(res[:, toks], r1[:, toks], r2[:, toks], ADD)
+            queue.dma_start(out=out[:, toks], in_=res[:, toks])

@@ -18,17 +18,18 @@ SILU = mybir.ActivationFunctionType.Silu
 
 P = 128
 J = 4
-LOADS = "offs xa xb w10 w30 w11 w31 pos w12 w32 w13 w33 w14 w34 w15 w35 w16 w36 w17 w37 w20 w24 w26 gate".split()
-GATHERS = ((0, 2), (2, 3), (5, 3))
-GATHER_AT = {0: 0, 1: 1, 3: 2}
-Y_GROUPS = ((0, 1, 2, 3), (4, 5), (6, 7))
-W2_GROUPS = ((0, 1, 2, 3), (4, 5), (6, 7))
-W2_AT = {8: ((0, 1, 2, 3), (4, 5), (6, 7))}
-W2_ON_VECTOR = (3, 5, 6, 7)
-V1 = {7: 64}
-S3 = {7: 48}
-SEPARATE = (7,)
-XV = (256, 256)
+LAST = E - 1
+W2_LOADS = ((0, 1), (2, 3), (4, 5), (6, 7))
+W2_LOAD_ON_VECTOR = (4, 5)
+W2_QUANT = ((0, 1), (2, 3), (4, 5, 6, 7))
+LISTS_AFTER = 1
+GATHERS = {0: (0, 2), 1: (2, 3), 2: (5, 3)}
+X_ON_VECTOR = 344
+W3_ON_SCALAR = 40
+LAST_W1_ON_SCALAR = 88
+LAST_W3_ON_SCALAR = 44
+JOINT = range(E - 1)
+H_GROUPS = ((0, 1), (2, 3), (4, 5), (6, 7))
 
 
 def tile_routed_moe_kernel(tc, xT, w1, w3, w2, gate, offs, pos1, pos2, out):
@@ -36,60 +37,48 @@ def tile_routed_moe_kernel(tc, xT, w1, w3, w2, gate, offs, pos1, pos2, out):
     with ExitStack() as ctx:
         held = ctx.enter_context(tc.tile_pool(name="held", bufs=1))
         stage = ctx.enter_context(tc.tile_pool(name="stage", bufs=2))
-        psum = ctx.enter_context(tc.psum_pool(name="psum", bufs=3))
+        psum = ctx.enter_context(tc.psum_pool(name="psum", bufs=1))
 
         offs_t = held.tile([P, SLOTS // 16], U16, name="offs_t")
         pos1_t = held.tile([P, T // 16], U16, name="pos1_t")
         pos2_t = held.tile([P, T // 16], U16, name="pos2_t")
-        x_raw = [held.tile([P, J, T // 2], F32, name=f"x_raw{h}") for h in range(2)]
+        x_raw = held.tile([P, J, T], F32, name="x_raw")
         gates = held.tile([P, 2, T], F32, name="gates")
-        w1_raw = [held.tile([P, J * H], F32, name=f"w1_raw{e}") for e in range(E)]
-        w3_raw = [held.tile([P, J * H], F32, name=f"w3_raw{e}") for e in range(E)]
-        w2_raw = {g: held.tile([P, len(g), J * N], F32, name=f"w2_raw{g[0]}") for g in W2_GROUPS}
+        w_raw = [[held.tile([P, J * H], F32, name=f"w_raw{u}_{e}", align_bytes=64) for e in range(E)] for u in range(2)]
+        w2_raw = {g: held.tile([P, len(g), J * N], F32, name=f"w2_raw{g[0]}", align_bytes=64) for g in W2_LOADS}
 
         warm = held.tile([P, 1], F32, name="warm")
         nc.vector.memset(warm[:], 0.0)
         nc.scalar.activation(warm[:], warm[:], SILU)
 
-        for name in LOADS:
-            if name == "offs":
-                nc.sync.dma_start(offs_t[:], offs)
-            elif name == "pos":
+        def load_w2(g):
+            nc.sync.dma_start(out=w2_raw[g][:], in_=w2[g[0]:g[-1] + 1, :, :].rearrange("e (p j) n -> p e (j n)", j=J))
+
+        nc.sync.dma_start(out=x_raw[:], in_=xT.rearrange("(p j) t -> p j t", j=J))
+        nc.sync.dma_start(offs_t[:], offs)
+        for e in range(E):
+            for u, w in enumerate((w1, w3)):
+                nc.sync.dma_start(out=w_raw[u][e][:], in_=w[e, :, :].rearrange("(p j) h -> p (j h)", j=J))
+            if e == LISTS_AFTER:
                 nc.sync.dma_start(pos1_t[:], pos1)
                 nc.sync.dma_start(pos2_t[:], pos2)
-            elif name[0] == "x":
-                h = "ab".index(name[1])
-                nc.sync.dma_start(out=x_raw[h][:], in_=xT[:, h * (T // 2):(h + 1) * (T // 2)].rearrange("(p j) t -> p j t", j=J))
-            elif name == "gate":
-                nc.sync.dma_start(out=gates[:], in_=gate.rearrange("g p t -> p g t"))
-            elif name[:2] == "w2":
-                for g in W2_GROUPS:
-                    if g[0] == int(name[2]):
-                        nc.sync.dma_start(out=w2_raw[g][:], in_=w2[g[0]:g[-1] + 1, :, :].rearrange("e (p j) n -> p e (j n)", j=J))
-            else:
-                e = int(name[2])
-                raw, w = (w1_raw[e], w1) if name[1] == "1" else (w3_raw[e], w3)
-                nc.sync.dma_start(out=raw[:], in_=w[e, :, :].rearrange("(p j) h -> p (j h)", j=J))
+        for g in W2_LOADS:
+            load_w2(g)
+        nc.sync.dma_start(out=gates[:], in_=gate.rearrange("g p t -> p g t"))
 
         x_codes = held.tile([P, T], U32, name="x_codes", align_bytes=64)
         x_scales = held.tile([P, T], U8, name="x_scales", align_bytes=64)
         nc.gpsimd.memset(x_scales[:], 0)
         x_grouped = held.tile([P, T * J], BF16, name="x_grouped", align_bytes=64)
-        for h in range(2):
-            x_src = x_raw[h][:].rearrange("p j (c i) -> p c j i", i=4)
-            x_dst = x_grouped[:, h * 1024:(h + 1) * 1024].rearrange("p (c i j) -> p c j i", i=4, j=J)
-            cut = XV[h] // 4
-            if cut < 64:
-                nc.scalar.copy(out=x_dst[:, cut:64], in_=x_src[:, cut:64])
-            if cut:
-                nc.vector.tensor_copy(out=x_dst[:, 0:cut], in_=x_src[:, 0:cut])
-            half = slice(h * (T // 2), (h + 1) * (T // 2))
-            nc.vector.quantize_mx(out=x_codes[:, half].bitcast(FP8X4), scales=x_scales[:, half],
-                                  in_=x_grouped[:, h * 1024:(h + 1) * 1024])
+        x_src = x_raw[:].rearrange("p j (c i) -> p c j i", i=4)
+        x_dst = x_grouped[:].rearrange("p (c i j) -> p c j i", i=4, j=J)
+        cut = X_ON_VECTOR // 4
+        nc.vector.tensor_copy(out=x_dst[:, 0:cut], in_=x_src[:, 0:cut])
+        nc.scalar.copy(out=x_dst[:, cut:], in_=x_src[:, cut:])
+        nc.vector.quantize_mx(out=x_codes[:].bitcast(FP8X4), scales=x_scales[:], in_=x_grouped[:])
 
         s_codes = held.tile([P, SLOTS], U32, name="s_codes", align_bytes=64)
         s_scales = held.tile([P, SLOTS], U8, name="s_scales", align_bytes=64)
-        y_sb = held.tile([P, SLOTS], F32, name="y_sb")
         live = {}
 
         def gather(first, count):
@@ -98,150 +87,121 @@ def tile_routed_moe_kernel(tc, xT, w1, w3, w2, gate, offs, pos1, pos2, out):
             nc.vector.tensor_copy(s_codes[:, cols], x_codes[:].indirect(lst))
             nc.vector.tensor_copy(s_scales[:, cols], x_scales[:].indirect(lst))
 
-        def up_views(raw, grouped, m0, m1):
-            src = raw[:].rearrange("p (j m t) -> p m j t", j=J, t=4)
-            dst = grouped.rearrange("p (t m j) -> p m j t", t=4, j=J)
-            return src[:, m0:m1], dst[:, m0:m1]
+        def inter(u, e, on_scalar):
+            if u == 0:
+                pool = held if e == LAST else stage
+                live["g", e] = pool.tile([P, 2, H * J], BF16, name="grouped", align_bytes=64)
+            src = w_raw[u][e][:].rearrange("p (j m t) -> p m j t", j=J, t=4)
+            dst = live["g", e][:, u, :].rearrange("p (t m j) -> p m j t", t=4, j=J)
+            cut = P - on_scalar
+            if cut:
+                nc.vector.tensor_copy(out=dst[:, 0:cut], in_=src[:, 0:cut])
+            nc.scalar.copy(out=dst[:, cut:], in_=src[:, cut:])
 
-        def inter(which, e):
-            if which == 0:
-                live["g", e] = stage.tile([P, 2, H * J], BF16, name="grouped", align_bytes=64)
-            raw = (w1_raw, w3_raw)[which][e]
-            v = V1.get(e, 0) if which == 0 else 128 - S3.get(e, 0)
-            parts = [(0, v, 128)]
-            for lo, cut, hi in parts:
-                if hi > cut:
-                    src, dst = up_views(raw, live["g", e][:, which, :], cut, hi)
-                    nc.scalar.copy(out=dst, in_=src)
-                if cut > lo:
-                    src, dst = up_views(raw, live["g", e][:, which, :], lo, cut)
-                    nc.vector.tensor_copy(out=dst, in_=src)
-
-        def products(which, e):
-            codes, scales = live["q", e]
-            acc = psum.tile([P, 4, C], F32, name=f"acc{which}", bufs=3)
+        def quant(us, e):
+            n = len(us)
+            codes = stage.tile([P, n * H], U32, name=f"codes{n}", align_bytes=64)
+            scales = stage.tile([P, n * H], U8, name=f"scales{n}", align_bytes=64)
+            nc.vector.quantize_mx(out=codes[:].bitcast(FP8X4), scales=scales[:],
+                                  in_=live["g", e][:, us[0]:us[-1] + 1, :].rearrange("p u k -> p (u k)"))
             cols = slice(e * C, (e + 1) * C)
-            for t in range(4):
-                blk = slice(which * H + t * P, which * H + (t + 1) * P)
-                nc.tensor.matmul_mx(
-                    out=acc[:, t, :], lhsT=codes[:, blk].bitcast(FP8X4), lhsT_scale=scales[:, blk],
-                    rhs=s_codes[:, cols].bitcast(FP8X4), rhs_scale=s_scales[:, cols], start=True, stop=True)
-            live["acc", which, e] = acc
-
-        def quant(whichs, e):
-            if whichs[0] == 0:
-                codes = stage.tile([P, 2 * H], U32, name="codes", align_bytes=64)
-                scales = stage.tile([P, 2 * H], U8, name="scales", align_bytes=64)
-                live["q", e] = codes, scales
-            codes, scales = live["q", e]
-            cols = slice(whichs[0] * H, (whichs[-1] + 1) * H)
-            words = slice(whichs[0] * H * J, (whichs[-1] + 1) * H * J)
-            nc.vector.quantize_mx(out=codes[:, cols].bitcast(FP8X4), scales=scales[:, cols],
-                                  in_=live["g", e][:].rearrange("p w k -> p (w k)")[:, words])
-            for which in whichs:
-                products(which, e)
+            for i, u in enumerate(us):
+                acc = psum.tile([P, 4, C], F32, name=f"acc{u}", bufs=2)
+                for t in range(4):
+                    blk = slice(i * H + t * P, i * H + (t + 1) * P)
+                    nc.tensor.matmul_mx(
+                        out=acc[:, t, :], lhsT=codes[:, blk].bitcast(FP8X4), lhsT_scale=scales[:, blk],
+                        rhs=s_codes[:, cols].bitcast(FP8X4), rhs_scale=s_scales[:, cols], start=True, stop=True)
+                live["acc", u, e] = acc
 
         def silu(e):
-            if e == E - 1:
-                sil = held.tile([P, C, 4], F32, name="sil_last", tag="last", align_bytes=64)
-            else:
-                sil = stage.tile([P, C, 4], F32, name="sil")
+            after = f"w_raw0_{LAST}" if e == LAST - 1 else f"w_raw1_{min(e + 1, LAST)}"
+            sil = held.tile([P, C, 4], F32, name=f"sil{e}", tag=after, align_bytes=64)
             nc.scalar.activation(sil[:], live["acc", 0, e][:].rearrange("p t c -> p c t"), SILU)
             live["sil", e] = sil
 
-        def inter2(g):
-            tag = "last" if g[-1] == E - 1 else f"grp2_{g[0]}"
-            grouped = held.tile([P, len(g), N * J], BF16, name=f"grp2_{g[0]}", tag=tag, align_bytes=64)
-            src = w2_raw[g][:].rearrange("p e (j c i) -> p e c j i", j=J, i=4)
-            dst = grouped[:].rearrange("p e (c i j) -> p e c j i", i=4, j=J)
-            on_vector = [e for e in g if e in W2_ON_VECTOR]
-            cut = on_vector[0] - g[0] if on_vector else len(g)
-            if cut:
-                nc.scalar.copy(out=dst[:, 0:cut], in_=src[:, 0:cut])
-            if cut < len(g):
-                nc.vector.tensor_copy(out=dst[:, cut:], in_=src[:, cut:])
+        def inter2(grp):
+            grouped = held.tile([P, len(grp), N * J], BF16, name=f"grp2_{grp[0]}", align_bytes=64)
+            for g in W2_LOADS:
+                if g[0] in grp:
+                    src = w2_raw[g][:].rearrange("p e (j c i) -> p e c j i", j=J, i=4)
+                    dst = grouped[:, g[0] - grp[0]:g[-1] + 1 - grp[0]].rearrange("p e (c i j) -> p e c j i", i=4, j=J)
+                    copy = nc.vector.tensor_copy if g == W2_LOAD_ON_VECTOR else nc.scalar.copy
+                    copy(out=dst, in_=src)
+            live["g2", grp] = grouped
+
+        def quant2(g):
             codes = held.tile([P, len(g), N], U32, name=f"cod2_{g[0]}", align_bytes=64)
             scales = held.tile([P, len(g), N], U8, name=f"scl2_{g[0]}", align_bytes=64)
             nc.vector.quantize_mx(
                 out=codes[:].rearrange("p e n -> p (e n)").bitcast(FP8X4),
-                scales=scales[:].rearrange("p e n -> p (e n)"), in_=grouped[:].rearrange("p e n -> p (e n)"))
+                scales=scales[:].rearrange("p e n -> p (e n)"), in_=live["g2", g][:].rearrange("p e n -> p (e n)"))
             for i, e in enumerate(g):
                 live["w2", e] = codes[:, i, :], scales[:, i, :]
 
-        h_group_of = {e: g for g in ((0, 1), (2, 3), (4, 5), (6,), (7,)) for e in g}
-        group_of = {e: g for g in Y_GROUPS for e in g}
+        h_group_of = {e: g for g in H_GROUPS for e in g}
 
         def hid(e):
             grp = h_group_of[e]
             if e == grp[0]:
-                live["hb", grp] = stage.tile([P, 2, C, 4], BF16, name="hb", align_bytes=64)
+                pool, tag = (held, "grouped") if grp[-1] == LAST else (stage, "hb")
+                live["hb", grp] = pool.tile([P, 2, C, 4], BF16, name="hb", tag=tag, align_bytes=64)
             nc.vector.tensor_tensor(live["hb", grp][:, e - grp[0]], live["acc", 1, e][:].rearrange("p t c -> p c t"), live["sil", e][:], MULT)
 
         def quanth(grp):
             n = len(grp)
-            codes = stage.tile([P, 2, C], U32, name="codh", align_bytes=64, bufs=E)
-            scales = stage.tile([P, 2, C], U8, name="sclh", align_bytes=64, bufs=E)
-            nc.vector.quantize_mx(out=codes[:, 0:n].rearrange("p e c -> p (e c)").bitcast(FP8X4),
-                                  scales=scales[:, 0:n].rearrange("p e c -> p (e c)"),
+            codes = held.tile([P, n, C], U32, name=f"codh{grp[0]}", align_bytes=64)
+            scales = held.tile([P, n, C], U8, name=f"sclh{grp[0]}", align_bytes=64)
+            nc.vector.quantize_mx(out=codes[:].rearrange("p e c -> p (e c)").bitcast(FP8X4),
+                                  scales=scales[:].rearrange("p e c -> p (e c)"),
                                   in_=live["hb", grp][:, 0:n].rearrange("p e c t -> p (e c t)"))
             for i, e in enumerate(grp):
                 live["qh", e] = codes[:, i, :], scales[:, i, :]
 
-        def down(e):
-            codes, scales = live["qh", e]
-            grp = group_of[e]
-            if e == grp[0]:
-                live["y", grp] = psum.tile([P, 4, C], F32, name="acc_y", bufs=2)
-            w2c, w2s = live["w2", e]
-            nc.tensor.matmul_mx(
-                out=live["y", grp][:, e - grp[0], :], lhsT=w2c.bitcast(FP8X4), lhsT_scale=w2s,
-                rhs=codes.bitcast(FP8X4), rhs_scale=scales, start=True, stop=True)
+        def down(grp, step, copy):
+            acc = psum.tile([P, len(grp), C], F32, name=f"acc_y{grp[0]}")
+            for i, e in enumerate(grp):
+                codes, scales = live["qh", e]
+                w2c, w2s = live["w2", e]
+                nc.tensor.matmul_mx(
+                    out=acc[:, i, :], lhsT=w2c.bitcast(FP8X4), lhsT_scale=w2s,
+                    rhs=codes.bitcast(FP8X4), rhs_scale=scales, start=True, stop=True)
+            copy(out=y_sb[:].rearrange("p (e c) -> p e c", c=C)[:, grp[0]:grp[-1] + 1:step, :], in_=acc[:])
 
-        def fetch(grp):
-            nc.scalar.copy(
-                out=y_sb[:, grp[0] * C:(grp[-1] + 1) * C].rearrange("p (g c) -> p g c", c=C),
-                in_=live["y", grp][:, 0:len(grp), :])
-
-        pending = []
-        for e in range(E + 1):
-            if e in GATHER_AT:
-                gather(*GATHERS[GATHER_AT[e]])
-            if e < E:
-                inter(0, e)
-                if e in SEPARATE:
-                    quant((0,), e)
-                    silu(e)
-                    if e > 0:
-                        hid(e - 1)
-                inter(1, e)
-            if 0 < e < E and e not in SEPARATE:
+        for e in range(E):
+            if e in GATHERS:
+                gather(*GATHERS[e])
+            inter(0, e, LAST_W1_ON_SCALAR if e == LAST else P)
+            if e == LAST:
+                quant((0,), e)
+                silu(e - 1)
+            inter(1, e, LAST_W3_ON_SCALAR if e == LAST else W3_ON_SCALAR)
+            quant((0, 1) if e in JOINT else (1,), e)
+            if 0 < e < LAST:
+                silu(e - 1)
                 hid(e - 1)
-            if e < E:
-                if e in SEPARATE:
-                    quant((1,), e)
-                else:
-                    quant((0, 1), e)
-                    silu(e)
-            if e == E:
-                hid(e - 1)
-            if e > 0:
                 if e - 1 == h_group_of[e - 1][-1]:
                     quanth(h_group_of[e - 1])
-                    pending.extend(h_group_of[e - 1])
-            for g in W2_AT.get(e, ()):
-                inter2(g)
-            for d in list(pending):
-                if ("w2", d) in live:
-                    down(d)
-                    pending.remove(d)
-                    if d == group_of[d][-1]:
-                        fetch(group_of[d])
+        silu(LAST)
+        hid(LAST - 1)
+        hid(LAST)
+        quanth(H_GROUPS[-1])
+        for grp in W2_QUANT:
+            inter2(grp)
+            quant2(grp)
+        y_sb = held.tile([P, SLOTS], F32, name="y_sb", tag=f"w2_raw{W2_LOADS[-1][0]}", align_bytes=64)
+        down((0, 1, 2, 3), 1, nc.scalar.copy)
+        down((4, 6), 2, nc.vector.tensor_copy)
+        down((5, 7), 2, nc.scalar.copy)
 
-        r1 = held.tile([P, T], F32, name="r1")
-        r2 = held.tile([P, T], F32, name="r2")
+        r1 = held.tile([P, T], F32, name="r1", tag="x_raw")
+        r2 = held.tile([P, T], F32, name="r2", tag="w_raw0_0", align_bytes=64)
         nc.vector.tensor_tensor(r1[:], y_sb[:].indirect(pos1_t[:]), gates[:, 0, :], MULT)
-        nc.vector.tensor_tensor(r2[:], y_sb[:].indirect(pos2_t[:]), gates[:, 1, :], MULT)
+        halves = [slice(h * T // 2, (h + 1) * T // 2) for h in range(2)]
+        for toks in halves:
+            lst = pos2_t[:, toks.start // 16:toks.stop // 16]
+            nc.vector.tensor_tensor(r2[:, toks], y_sb[:].indirect(lst), gates[:, 1, toks], MULT)
         res = held.tile([P, T], F32, name="res")
-        for queue, toks in ((nc.sync, slice(0, T // 2)), (nc.scalar, slice(T // 2, T))):
+        for queue, toks in zip((nc.sync, nc.scalar), halves):
             nc.vector.tensor_tensor(res[:, toks], r1[:, toks], r2[:, toks], ADD)
             queue.dma_start(out=out[:, toks], in_=res[:, toks])

@@ -20,8 +20,7 @@ P = 128
 J = 4
 LAST = E - 1
 W2_LOADS = ((0, 1), (2, 3), (4, 5), (6, 7))
-W2_LOAD_ON_VECTOR = (4, 5)
-W2_QUANT = ((0, 1), (2, 3), (4, 5, 6, 7))
+W2_ON_VECTOR = (5, 7)
 LISTS_AFTER = 1
 GATHERS = {0: (0, 2), 1: (2, 3), 2: (5, 3)}
 X_ON_VECTOR = 344
@@ -89,8 +88,7 @@ def tile_routed_moe_kernel(tc, xT, w1, w3, w2, gate, offs, pos1, pos2, out):
 
         def inter(u, e, on_scalar):
             if u == 0:
-                pool = held if e == LAST else stage
-                live["g", e] = pool.tile([P, 2, H * J], BF16, name="grouped", align_bytes=64)
+                live["g", e] = stage.tile([P, 2, H * J], BF16, name="grouped", align_bytes=64)
             src = w_raw[u][e][:].rearrange("p (j m t) -> p m j t", j=J, t=4)
             dst = live["g", e][:, u, :].rearrange("p (t m j) -> p m j t", t=4, j=J)
             cut = P - on_scalar
@@ -120,15 +118,16 @@ def tile_routed_moe_kernel(tc, xT, w1, w3, w2, gate, offs, pos1, pos2, out):
             nc.scalar.activation(sil[:], live["acc", 0, e][:].rearrange("p t c -> p c t"), SILU)
             live["sil", e] = sil
 
-        def inter2(grp):
-            grouped = held.tile([P, len(grp), N * J], BF16, name=f"grp2_{grp[0]}", align_bytes=64)
-            for g in W2_LOADS:
-                if g[0] in grp:
-                    src = w2_raw[g][:].rearrange("p e (j c i) -> p e c j i", j=J, i=4)
-                    dst = grouped[:, g[0] - grp[0]:g[-1] + 1 - grp[0]].rearrange("p e (c i j) -> p e c j i", i=4, j=J)
-                    copy = nc.vector.tensor_copy if g == W2_LOAD_ON_VECTOR else nc.scalar.copy
-                    copy(out=dst, in_=src)
-            live["g2", grp] = grouped
+        def inter2(g):
+            grouped = held.tile([P, len(g), N * J], BF16, name=f"grp2_{g[0]}", align_bytes=64)
+            src = w2_raw[g][:].rearrange("p e (j c i) -> p e c j i", j=J, i=4)
+            dst = grouped[:].rearrange("p e (c i j) -> p e c j i", i=4, j=J)
+            if g[1] in W2_ON_VECTOR:
+                nc.scalar.copy(out=dst[:, 0], in_=src[:, 0])
+                nc.vector.tensor_copy(out=dst[:, 1], in_=src[:, 1])
+            else:
+                nc.scalar.copy(out=dst, in_=src)
+            live["g2", g] = grouped
 
         def quant2(g):
             codes = held.tile([P, len(g), N], U32, name=f"cod2_{g[0]}", align_bytes=64)
@@ -144,8 +143,7 @@ def tile_routed_moe_kernel(tc, xT, w1, w3, w2, gate, offs, pos1, pos2, out):
         def hid(e):
             grp = h_group_of[e]
             if e == grp[0]:
-                pool, tag = (held, "grouped") if grp[-1] == LAST else (stage, "hb")
-                live["hb", grp] = pool.tile([P, 2, C, 4], BF16, name="hb", tag=tag, align_bytes=64)
+                live["hb", grp] = stage.tile([P, 2, C, 4], BF16, name="hb", align_bytes=64)
             nc.vector.tensor_tensor(live["hb", grp][:, e - grp[0]], live["acc", 1, e][:].rearrange("p t c -> p c t"), live["sil", e][:], MULT)
 
         def quanth(grp):
@@ -175,6 +173,7 @@ def tile_routed_moe_kernel(tc, xT, w1, w3, w2, gate, offs, pos1, pos2, out):
             if e == LAST:
                 quant((0,), e)
                 silu(e - 1)
+                hid(e - 1)
             inter(1, e, LAST_W3_ON_SCALAR if e == LAST else W3_ON_SCALAR)
             quant((0, 1) if e in JOINT else (1,), e)
             if 0 < e < LAST:
@@ -183,10 +182,9 @@ def tile_routed_moe_kernel(tc, xT, w1, w3, w2, gate, offs, pos1, pos2, out):
                 if e - 1 == h_group_of[e - 1][-1]:
                     quanth(h_group_of[e - 1])
         silu(LAST)
-        hid(LAST - 1)
         hid(LAST)
         quanth(H_GROUPS[-1])
-        for grp in W2_QUANT:
+        for grp in W2_LOADS:
             inter2(grp)
             quant2(grp)
         y_sb = held.tile([P, SLOTS], F32, name="y_sb", tag=f"w2_raw{W2_LOADS[-1][0]}", align_bytes=64)

@@ -19,9 +19,9 @@ SILU = mybir.ActivationFunctionType.Silu
 P = 128
 J = 4
 LAST = E - 1
-W2_LOADS = ((0, 1), (2, 3), (4, 5), (6, 7))
+W2_LOADS = ((0, 1), (2, 3), (4, 5), (6,), (7,))
 W2_ON_VECTOR = (5, 7)
-LISTS_AFTER = 1
+FIRST_PART = 384
 GATHERS = {0: (0, 2), 1: (2, 3), 2: (5, 3)}
 X_ON_VECTOR = 344
 W3_ON_SCALAR = 40
@@ -42,7 +42,7 @@ def tile_routed_moe_kernel(tc, xT, w1, w3, w2, gate, offs, pos1, pos2, out):
         pos1_t = held.tile([P, T // 16], U16, name="pos1_t")
         pos2_t = held.tile([P, T // 16], U16, name="pos2_t")
         x_raw = held.tile([P, J, T], F32, name="x_raw")
-        gates = held.tile([P, 2, T], F32, name="gates")
+        gates = [held.tile([P, T], F32, name=f"gate{g}") for g in range(2)]
         w_raw = [[held.tile([P, J * H], F32, name=f"w_raw{u}_{e}", align_bytes=64) for e in range(E)] for u in range(2)]
         w2_raw = {g: held.tile([P, len(g), J * N], F32, name=f"w2_raw{g[0]}", align_bytes=64) for g in W2_LOADS}
 
@@ -58,12 +58,11 @@ def tile_routed_moe_kernel(tc, xT, w1, w3, w2, gate, offs, pos1, pos2, out):
         for e in range(E):
             for u, w in enumerate((w1, w3)):
                 nc.sync.dma_start(out=w_raw[u][e][:], in_=w[e, :, :].rearrange("(p j) h -> p (j h)", j=J))
-            if e == LISTS_AFTER:
-                nc.sync.dma_start(pos1_t[:], pos1)
-                nc.sync.dma_start(pos2_t[:], pos2)
         for g in W2_LOADS:
             load_w2(g)
-        nc.sync.dma_start(out=gates[:], in_=gate.rearrange("g p t -> p g t"))
+        for lst, pos, g in ((pos1_t, pos1, 0), (pos2_t, pos2, 1)):
+            nc.sync.dma_start(lst[:], pos)
+            nc.sync.dma_start(out=gates[g][:], in_=gate[g, :, :])
 
         x_codes = held.tile([P, T], U32, name="x_codes", align_bytes=64)
         x_scales = held.tile([P, T], U8, name="x_scales", align_bytes=64)
@@ -122,11 +121,11 @@ def tile_routed_moe_kernel(tc, xT, w1, w3, w2, gate, offs, pos1, pos2, out):
             grouped = held.tile([P, len(g), N * J], BF16, name=f"grp2_{g[0]}", align_bytes=64)
             src = w2_raw[g][:].rearrange("p e (j c i) -> p e c j i", j=J, i=4)
             dst = grouped[:].rearrange("p e (c i j) -> p e c j i", i=4, j=J)
-            if g[1] in W2_ON_VECTOR:
-                nc.scalar.copy(out=dst[:, 0], in_=src[:, 0])
-                nc.vector.tensor_copy(out=dst[:, 1], in_=src[:, 1])
-            else:
-                nc.scalar.copy(out=dst, in_=src)
+            cut = len(g) - (g[-1] in W2_ON_VECTOR)
+            if cut:
+                nc.scalar.copy(out=dst[:, 0:cut], in_=src[:, 0:cut])
+            if cut < len(g):
+                nc.vector.tensor_copy(out=dst[:, cut], in_=src[:, cut])
             live["g2", g] = grouped
 
         def quant2(g):
@@ -156,7 +155,7 @@ def tile_routed_moe_kernel(tc, xT, w1, w3, w2, gate, offs, pos1, pos2, out):
             for i, e in enumerate(grp):
                 live["qh", e] = codes[:, i, :], scales[:, i, :]
 
-        def down(grp, step, copy):
+        def down(grp):
             acc = psum.tile([P, len(grp), C], F32, name=f"acc_y{grp[0]}")
             for i, e in enumerate(grp):
                 codes, scales = live["qh", e]
@@ -164,7 +163,7 @@ def tile_routed_moe_kernel(tc, xT, w1, w3, w2, gate, offs, pos1, pos2, out):
                 nc.tensor.matmul_mx(
                     out=acc[:, i, :], lhsT=w2c.bitcast(FP8X4), lhsT_scale=w2s,
                     rhs=codes.bitcast(FP8X4), rhs_scale=scales, start=True, stop=True)
-            copy(out=y_sb[:].rearrange("p (e c) -> p e c", c=C)[:, grp[0]:grp[-1] + 1:step, :], in_=acc[:])
+            nc.scalar.copy(out=y_sb[:, grp[0] * C:(grp[-1] + 1) * C], in_=acc[:].rearrange("p e c -> p (e c)"))
 
         for e in range(E):
             if e in GATHERS:
@@ -187,19 +186,24 @@ def tile_routed_moe_kernel(tc, xT, w1, w3, w2, gate, offs, pos1, pos2, out):
         for grp in W2_LOADS:
             inter2(grp)
             quant2(grp)
-        y_sb = held.tile([P, SLOTS], F32, name="y_sb", tag=f"w2_raw{W2_LOADS[-1][0]}", align_bytes=64)
-        down((0, 1, 2, 3), 1, nc.scalar.copy)
-        down((4, 6), 2, nc.vector.tensor_copy)
-        down((5, 7), 2, nc.scalar.copy)
+        y_sb = held.tile([P, SLOTS], F32, name="y_sb", tag=f"w2_raw{W2_LOADS[-2][0]}", align_bytes=64)
+        for grp in ((0, 1, 2, 3), (4, 5, 6), (7,)):
+            down(grp)
 
         r1 = held.tile([P, T], F32, name="r1", tag="x_raw")
         r2 = held.tile([P, T], F32, name="r2", tag="w_raw0_0", align_bytes=64)
-        nc.vector.tensor_tensor(r1[:], y_sb[:].indirect(pos1_t[:]), gates[:, 0, :], MULT)
-        halves = [slice(h * T // 2, (h + 1) * T // 2) for h in range(2)]
-        for toks in halves:
-            lst = pos2_t[:, toks.start // 16:toks.stop // 16]
-            nc.vector.tensor_tensor(r2[:, toks], y_sb[:].indirect(lst), gates[:, 1, toks], MULT)
         res = held.tile([P, T], F32, name="res")
-        for queue, toks in zip((nc.sync, nc.scalar), halves):
+
+        def fetch(r, lst, g, toks):
+            nc.vector.tensor_tensor(r[:, toks], y_sb[:].indirect(lst[:, toks.start // 16:toks.stop // 16]), gates[g][:, toks], MULT)
+
+        def finish(queue, toks):
             nc.vector.tensor_tensor(res[:, toks], r1[:, toks], r2[:, toks], ADD)
             queue.dma_start(out=out[:, toks], in_=res[:, toks])
+
+        first, second = slice(0, FIRST_PART), slice(FIRST_PART, T)
+        fetch(r1, pos1_t, 0, slice(0, T))
+        fetch(r2, pos2_t, 1, first)
+        fetch(r2, pos2_t, 1, second)
+        finish(nc.sync, first)
+        finish(nc.scalar, second)

@@ -24,11 +24,10 @@ W2_ON_VECTOR = (5, 7)
 FIRST_PART = 384
 GATHERS = {0: (0, 2), 1: (2, 3), 2: (5, 3)}
 X_ON_VECTOR = 344
-W3_ON_SCALAR = 40
+W3_ON_SCALAR = {E - 2: 40, E - 1: 50}
 LAST_W1_ON_SCALAR = 88
-LAST_W3_ON_SCALAR = 44
 JOINT = range(E - 1)
-H_GROUPS = ((0, 1), (2, 3), (4, 5), (6, 7))
+H_GROUPS = ((0,), (1, 2), (3, 4), (5, 6), (7,))
 
 
 def tile_routed_moe_kernel(tc, xT, w1, w3, w2, gate, offs, pos1, pos2, out):
@@ -77,6 +76,7 @@ def tile_routed_moe_kernel(tc, xT, w1, w3, w2, gate, offs, pos1, pos2, out):
 
         s_codes = held.tile([P, SLOTS], U32, name="s_codes", align_bytes=64)
         s_scales = held.tile([P, SLOTS], U8, name="s_scales", align_bytes=64)
+        last_stage = held.tile([P, 2 * H * J + 4 * C], BF16, name="last_stage", align_bytes=64)
         live = {}
 
         def gather(first, count):
@@ -87,20 +87,25 @@ def tile_routed_moe_kernel(tc, xT, w1, w3, w2, gate, offs, pos1, pos2, out):
 
         def inter(u, e, on_scalar):
             if u == 0:
-                live["g", e] = stage.tile([P, 2, H * J], BF16, name="grouped", align_bytes=64)
+                if e == LAST:
+                    live["g", e] = [last_stage[:, 0:H * J], last_stage[:, H * J + 4 * C:]]
+                else:
+                    grouped = stage.tile([P, 2, H * J], BF16, name="grouped", align_bytes=64)
+                    live["g", e] = [grouped[:, 0, :], grouped[:, 1, :], grouped[:].rearrange("p u k -> p (u k)")]
             src = w_raw[u][e][:].rearrange("p (j m t) -> p m j t", j=J, t=4)
-            dst = live["g", e][:, u, :].rearrange("p (t m j) -> p m j t", t=4, j=J)
+            dst = live["g", e][u].rearrange("p (t m j) -> p m j t", t=4, j=J)
             cut = P - on_scalar
             if cut:
                 nc.vector.tensor_copy(out=dst[:, 0:cut], in_=src[:, 0:cut])
-            nc.scalar.copy(out=dst[:, cut:], in_=src[:, cut:])
+            if on_scalar:
+                nc.scalar.copy(out=dst[:, cut:], in_=src[:, cut:])
 
         def quant(us, e):
             n = len(us)
             codes = stage.tile([P, n * H], U32, name=f"codes{n}", align_bytes=64)
             scales = stage.tile([P, n * H], U8, name=f"scales{n}", align_bytes=64)
             nc.vector.quantize_mx(out=codes[:].bitcast(FP8X4), scales=scales[:],
-                                  in_=live["g", e][:, us[0]:us[-1] + 1, :].rearrange("p u k -> p (u k)"))
+                                  in_=live["g", e][us[0] if n == 1 else 2])
             cols = slice(e * C, (e + 1) * C)
             for i, u in enumerate(us):
                 acc = psum.tile([P, 4, C], F32, name=f"acc{u}", bufs=2)
@@ -142,7 +147,11 @@ def tile_routed_moe_kernel(tc, xT, w1, w3, w2, gate, offs, pos1, pos2, out):
         def hid(e):
             grp = h_group_of[e]
             if e == grp[0]:
-                live["hb", grp] = stage.tile([P, 2, C, 4], BF16, name="hb", align_bytes=64)
+                if grp[-1] == LAST - 1:
+                    live["hb", grp] = last_stage[:, H * J:H * J + 8 * C].rearrange("p (e c t) -> p e c t", e=2, t=4)
+                else:
+                    hb = stage.tile([P, 2, C, 4], BF16, name="hb", align_bytes=64)
+                    live["hb", grp] = hb[:]
             nc.vector.tensor_tensor(live["hb", grp][:, e - grp[0]], live["acc", 1, e][:].rearrange("p t c -> p c t"), live["sil", e][:], MULT)
 
         def quanth(grp):
@@ -172,8 +181,7 @@ def tile_routed_moe_kernel(tc, xT, w1, w3, w2, gate, offs, pos1, pos2, out):
             if e == LAST:
                 quant((0,), e)
                 silu(e - 1)
-                hid(e - 1)
-            inter(1, e, LAST_W3_ON_SCALAR if e == LAST else W3_ON_SCALAR)
+            inter(1, e, W3_ON_SCALAR.get(e, 0))
             quant((0, 1) if e in JOINT else (1,), e)
             if 0 < e < LAST:
                 silu(e - 1)
@@ -181,7 +189,9 @@ def tile_routed_moe_kernel(tc, xT, w1, w3, w2, gate, offs, pos1, pos2, out):
                 if e - 1 == h_group_of[e - 1][-1]:
                     quanth(h_group_of[e - 1])
         silu(LAST)
+        hid(LAST - 1)
         hid(LAST)
+        quanth(H_GROUPS[-2])
         quanth(H_GROUPS[-1])
         for grp in W2_LOADS:
             inter2(grp)

@@ -45,10 +45,6 @@ def tile_routed_moe_kernel(tc, xT, w1, w3, w2, gate, offs, pos1, pos2, out):
         w_raw = [[held.tile([P, J * H], F32, name=f"w_raw{u}_{e}", align_bytes=64) for e in range(E)] for u in range(2)]
         w2_raw = {g: held.tile([P, len(g), J * N], F32, name=f"w2_raw{g[0]}", align_bytes=64) for g in W2_LOADS}
 
-        warm = held.tile([P, 1], F32, name="warm")
-        nc.vector.memset(warm[:], 0.0)
-        nc.scalar.activation(warm[:], warm[:], SILU)
-
         def load_w2(g):
             nc.sync.dma_start(out=w2_raw[g][:], in_=w2[g[0]:g[-1] + 1, :, :].rearrange("e (p j) n -> p e (j n)", j=J))
 

@@ -18,6 +18,7 @@ SILU = mybir.ActivationFunctionType.Silu
 
 P = 128
 J = 4
+DMA_ALIGN = 256
 LAST = E - 1
 W2_LOADS = ((0, 1), (2, 3), (4, 5), (6,), (7,))
 W2_ON_VECTOR = (5, 7)
@@ -40,10 +41,10 @@ def tile_routed_moe_kernel(tc, xT, w1, w3, w2, gate, offs, pos1, pos2, out):
         offs_t = held.tile([P, SLOTS // 16], U16, name="offs_t")
         pos1_t = held.tile([P, T // 16], U16, name="pos1_t")
         pos2_t = held.tile([P, T // 16], U16, name="pos2_t")
-        x_raw = held.tile([P, J, T], F32, name="x_raw")
-        gates = [held.tile([P, T], F32, name=f"gate{g}") for g in range(2)]
-        w_raw = [[held.tile([P, J * H], F32, name=f"w_raw{u}_{e}", align_bytes=64) for e in range(E)] for u in range(2)]
-        w2_raw = {g: held.tile([P, len(g), J * N], F32, name=f"w2_raw{g[0]}", align_bytes=64) for g in W2_LOADS}
+        x_raw = held.tile([P, J, T], F32, name="x_raw", align_bytes=DMA_ALIGN)
+        gates = [held.tile([P, T], F32, name=f"gate{g}", align_bytes=DMA_ALIGN) for g in range(2)]
+        w_raw = [[held.tile([P, J * H], F32, name=f"w_raw{u}_{e}", align_bytes=DMA_ALIGN) for e in range(E)] for u in range(2)]
+        w2_raw = {g: held.tile([P, len(g), J * N], F32, name=f"w2_raw{g[0]}", align_bytes=DMA_ALIGN) for g in W2_LOADS}
 
         def load_w2(g):
             nc.sync.dma_start(out=w2_raw[g][:], in_=w2[g[0]:g[-1] + 1, :, :].rearrange("e (p j) n -> p e (j n)", j=J))
@@ -114,7 +115,7 @@ def tile_routed_moe_kernel(tc, xT, w1, w3, w2, gate, offs, pos1, pos2, out):
 
         def silu(e):
             after = f"w_raw0_{LAST}" if e == LAST - 1 else f"w_raw1_{min(e + 1, LAST)}"
-            sil = held.tile([P, C, 4], F32, name=f"sil{e}", tag=after, align_bytes=64)
+            sil = held.tile([P, C, 4], F32, name=f"sil{e}", tag=after, align_bytes=DMA_ALIGN)
             nc.scalar.activation(sil[:], live["acc", 0, e][:].rearrange("p t c -> p c t"), SILU)
             live["sil", e] = sil
 
@@ -192,13 +193,13 @@ def tile_routed_moe_kernel(tc, xT, w1, w3, w2, gate, offs, pos1, pos2, out):
         for grp in W2_LOADS:
             inter2(grp)
             quant2(grp)
-        y_sb = held.tile([P, SLOTS], F32, name="y_sb", tag=f"w2_raw{W2_LOADS[-2][0]}", align_bytes=64)
+        y_sb = held.tile([P, SLOTS], F32, name="y_sb", tag=f"w2_raw{W2_LOADS[-2][0]}", align_bytes=DMA_ALIGN)
         for grp in ((0, 1, 2, 3), (4, 5, 6), (7,)):
             down(grp)
 
-        r1 = held.tile([P, T], F32, name="r1", tag="x_raw")
-        r2 = held.tile([P, T], F32, name="r2", tag="w_raw0_0", align_bytes=64)
-        res = held.tile([P, T], F32, name="res")
+        r1 = held.tile([P, T], F32, name="r1", tag="x_raw", align_bytes=DMA_ALIGN)
+        r2 = held.tile([P, T], F32, name="r2", tag="w_raw0_0", align_bytes=DMA_ALIGN)
+        res = held.tile([P, T], F32, name="res", tag="w_raw0_1", align_bytes=DMA_ALIGN)
 
         def fetch(r, lst, g, toks):
             nc.vector.tensor_tensor(r[:, toks], y_sb[:].indirect(lst[:, toks.start // 16:toks.stop // 16]), gates[g][:, toks], MULT)

@@ -15,6 +15,7 @@ FP8X4 = mybir.dt.float8_e4m3fn_x4
 MULT = mybir.AluOpType.mult
 ADD = mybir.AluOpType.add
 SILU = mybir.ActivationFunctionType.Silu
+COPY = mybir.ActivationFunctionType.Copy
 
 P = 128
 J = 4
@@ -201,16 +202,13 @@ def tile_routed_moe_kernel(tc, xT, w1, w3, w2, gate, offs, pos1, pos2, out):
         r2 = held.tile([P, T], F32, name="r2", tag="w_raw0_0", align_bytes=DMA_ALIGN)
         res = held.tile([P, T], F32, name="res", tag="w_raw0_1", align_bytes=DMA_ALIGN)
 
-        def fetch(r, lst, g, toks):
-            nc.vector.tensor_tensor(r[:, toks], y_sb[:].indirect(lst[:, toks.start // 16:toks.stop // 16]), gates[g][:, toks], MULT)
-
-        def finish(queue, toks):
-            nc.vector.tensor_tensor(res[:, toks], r1[:, toks], r2[:, toks], ADD)
+        p2 = held.tile([P, T], F32, name="p2", tag="w_raw0_2", align_bytes=DMA_ALIGN)
+        parts = slice(0, FIRST_PART), slice(FIRST_PART, T)
+        nc.vector.tensor_tensor(r1[:], y_sb[:].indirect(pos1_t[:]), gates[0][:], MULT)
+        for toks in parts:
+            nc.scalar.activation(r2[:, toks], y_sb[:].indirect(pos2_t[:, toks.start // 16:toks.stop // 16]), COPY)
+        for toks in parts:
+            nc.vector.tensor_tensor(p2[:, toks], r2[:, toks], gates[1][:, toks], MULT)
+        for queue, toks in zip((nc.sync, nc.scalar), parts):
+            nc.vector.tensor_tensor(res[:, toks], r1[:, toks], p2[:, toks], ADD)
             queue.dma_start(out=out[:, toks], in_=res[:, toks])
-
-        first, second = slice(0, FIRST_PART), slice(FIRST_PART, T)
-        fetch(r1, pos1_t, 0, slice(0, T))
-        fetch(r2, pos2_t, 1, first)
-        fetch(r2, pos2_t, 1, second)
-        finish(nc.sync, first)
-        finish(nc.scalar, second)

@@ -23,7 +23,7 @@ DMA_ALIGN = 256
 LAST = E - 1
 W2_LOADS = ((0, 1), (2, 3), (4, 5), (6,), (7,))
 W2_ON_VECTOR = (5, 7)
-FIRST_PART = 384
+FIRST_PART = 256
 GATHERS = {0: (0, 2), 1: (2, 3), 2: (5, 3)}
 X_ON_VECTOR = 344
 W3_ON_SCALAR = {E - 2: 40, E - 1: 50}
@@ -170,7 +170,8 @@ def tile_routed_moe_kernel(tc, xT, w1, w3, w2, gate, offs, pos1, pos2, out):
                 nc.tensor.matmul_mx(
                     out=acc[:, i, :], lhsT=w2c.bitcast(FP8X4), lhsT_scale=w2s,
                     rhs=codes.bitcast(FP8X4), rhs_scale=scales, start=True, stop=True)
-            nc.scalar.copy(out=y_sb[:, grp[0] * C:(grp[-1] + 1) * C], in_=acc[:].rearrange("p e c -> p (e c)"))
+            copy = nc.vector.tensor_copy if grp[-1] == LAST else nc.scalar.copy
+            copy(out=y_sb[:, grp[0] * C:(grp[-1] + 1) * C], in_=acc[:].rearrange("p e c -> p (e c)"))
 
         for e in range(E):
             if e in GATHERS:
@@ -195,7 +196,7 @@ def tile_routed_moe_kernel(tc, xT, w1, w3, w2, gate, offs, pos1, pos2, out):
             inter2(grp)
             quant2(grp)
         y_sb = held.tile([P, SLOTS], F32, name="y_sb", tag=f"w2_raw{W2_LOADS[-2][0]}", align_bytes=DMA_ALIGN)
-        for grp in ((0, 1, 2, 3), (4, 5, 6), (7,)):
+        for grp in ((0, 1, 2, 3), (4, 5), (6,), (7,)):
             down(grp)
 
         r1 = held.tile([P, T], F32, name="r1", tag="x_raw", align_bytes=DMA_ALIGN)

@@ -22,12 +22,12 @@ J = 4
 DMA_ALIGN = 256
 LAST = E - 1
 W2_LOADS = ((0, 1), (2, 3), (4, 5), (6,), (7,))
-W2_ON_VECTOR = (5, 7)
+W2_ON_VECTOR = (1, 5, 7)
 FIRST_PART = 256
 GATHERS = {0: (0, 2), 1: (2, 3), 2: (5, 3)}
 X_ON_VECTOR = 344
 W3_ON_SCALAR = {E - 2: 40, E - 1: 50}
-LAST_W1_ON_SCALAR = 88
+LAST_W1_ON_SCALAR = 80
 JOINT = range(E - 1)
 H_GROUPS = ((0,), (1, 2), (3, 4), (5, 6), (7,))
 

@@ -22,14 +22,15 @@ J = 4
 DMA_ALIGN = 256
 LAST = E - 1
 W2_LOADS = ((0, 1), (2, 3), (4, 5), (6,), (7,))
-W2_ON_VECTOR = (1, 5, 7)
+W2_ON_VECTOR = (0, 1, 5, 7)
+SHARED = (E - 2, E - 1)
+ROW = J * H
+LAP = 16
+PIECE = C * 4 // 2
 FIRST_PART = 256
 GATHERS = {0: (0, 2), 1: (2, 3), 2: (5, 3)}
 X_ON_VECTOR = 344
-W3_ON_SCALAR = {E - 2: 40, E - 1: 50}
-LAST_W1_ON_SCALAR = 80
-JOINT = range(E - 1)
-H_GROUPS = ((0,), (1, 2), (3, 4), (5, 6), (7,))
+ON_SCALAR = (64, 48)
 
 
 def tile_routed_moe_kernel(tc, xT, w1, w3, w2, gate, offs, pos1, pos2, out):
@@ -44,19 +45,20 @@ def tile_routed_moe_kernel(tc, xT, w1, w3, w2, gate, offs, pos1, pos2, out):
         pos2_t = held.tile([P, T // 16], U16, name="pos2_t")
         x_raw = held.tile([P, J, T], F32, name="x_raw", align_bytes=DMA_ALIGN)
         gates = [held.tile([P, T], F32, name=f"gate{g}", align_bytes=DMA_ALIGN) for g in range(2)]
-        w_raw = [[held.tile([P, J * H], F32, name=f"w_raw{u}_{e}", align_bytes=DMA_ALIGN) for e in range(E)] for u in range(2)]
+        ahead = {(1, LAST - 1): 2 * PIECE, (0, LAST): 3 * PIECE}
+        behind = {(1, LAST - 1): 2 * PIECE, (1, LAST): 2 * PIECE}
+        w_tile = {(u, e): held.tile([P, ahead.get((u, e), 0) + ROW + behind.get((u, e), 0)], F32, name=f"w_raw{u}_{e}", align_bytes=DMA_ALIGN)
+                  for e in range(E) for u in range(2)}
+        w_raw = {k: t[:, ahead.get(k, 0):ahead.get(k, 0) + ROW] for k, t in w_tile.items()}
         w2_raw = {g: held.tile([P, len(g), J * N], F32, name=f"w2_raw{g[0]}", align_bytes=DMA_ALIGN) for g in W2_LOADS}
-
-        def load_w2(g):
-            nc.sync.dma_start(out=w2_raw[g][:], in_=w2[g[0]:g[-1] + 1, :, :].rearrange("e (p j) n -> p e (j n)", j=J))
 
         nc.sync.dma_start(out=x_raw[:], in_=xT.rearrange("(p j) t -> p j t", j=J))
         nc.sync.dma_start(offs_t[:], offs)
         for e in range(E):
             for u, w in enumerate((w1, w3)):
-                nc.sync.dma_start(out=w_raw[u][e][:], in_=w[e, :, :].rearrange("(p j) h -> p (j h)", j=J))
+                nc.sync.dma_start(out=w_raw[u, e], in_=w[e, :, :].rearrange("(p j) h -> p (j h)", j=J))
         for g in W2_LOADS:
-            load_w2(g)
+            nc.sync.dma_start(out=w2_raw[g][:], in_=w2[g[0]:g[-1] + 1, :, :].rearrange("e (p j) n -> p e (j n)", j=J))
         for lst, pos, g in ((pos1_t, pos1, 0), (pos2_t, pos2, 1)):
             nc.sync.dma_start(lst[:], pos)
             nc.sync.dma_start(out=gates[g][:], in_=gate[g, :, :])
@@ -74,7 +76,12 @@ def tile_routed_moe_kernel(tc, xT, w1, w3, w2, gate, offs, pos1, pos2, out):
 
         s_codes = held.tile([P, SLOTS], U32, name="s_codes", align_bytes=64)
         s_scales = held.tile([P, SLOTS], U8, name="s_scales", align_bytes=64)
-        last_stage = held.tile([P, 2 * H * J + 4 * C], BF16, name="last_stage", align_bytes=64)
+        h_early = held.tile([P, 4, C * 4], BF16, name="h_early", align_bytes=64)
+        h_mid = w_tile[1, LAST - 1][:, LAP:LAP + 2 * PIECE].bitcast(BF16)
+        late = w_tile[0, LAST][:, LAP:LAP + 3 * PIECE].bitcast(BF16)
+        h_of = {e: h_early[:, e, :] for e in range(4)}
+        h_of[4], h_of[5] = h_mid[:, 0:4 * C], h_mid[:, 4 * C:]
+        h_of[LAST], h_of[LAST - 1] = late[:, 4 * C:8 * C], late[:, 8 * C:]
         live = {}
 
         def gather(first, count):
@@ -83,27 +90,23 @@ def tile_routed_moe_kernel(tc, xT, w1, w3, w2, gate, offs, pos1, pos2, out):
             nc.vector.tensor_copy(s_codes[:, cols], x_codes[:].indirect(lst))
             nc.vector.tensor_copy(s_scales[:, cols], x_scales[:].indirect(lst))
 
-        def inter(u, e, on_scalar):
+        def round_w(u, e, on_scalar):
             if u == 0:
-                if e == LAST:
-                    live["g", e] = [last_stage[:, 0:H * J], last_stage[:, H * J + 4 * C:]]
-                else:
-                    grouped = stage.tile([P, 2, H * J], BF16, name="grouped", align_bytes=64)
-                    live["g", e] = [grouped[:, 0, :], grouped[:, 1, :], grouped[:].rearrange("p u k -> p (u k)")]
-            src = w_raw[u][e][:].rearrange("p (j m t) -> p m j t", j=J, t=4)
-            dst = live["g", e][u].rearrange("p (t m j) -> p m j t", t=4, j=J)
+                live["g", e] = stage.tile([P, 2, H * J], BF16, name="grouped", align_bytes=64)
+            src = w_raw[u, e].rearrange("p (j m t) -> p m j t", j=J, t=4)
+            dst = live["g", e][:, u, :].rearrange("p (t m j) -> p m j t", t=4, j=J)
             cut = P - on_scalar
             if cut:
                 nc.vector.tensor_copy(out=dst[:, 0:cut], in_=src[:, 0:cut])
             if on_scalar:
                 nc.scalar.copy(out=dst[:, cut:], in_=src[:, cut:])
 
-        def quant(us, e):
+        def first_layer(us, e):
             n = len(us)
             codes = stage.tile([P, n * H], U32, name=f"codes{n}", align_bytes=64)
             scales = stage.tile([P, n * H], U8, name=f"scales{n}", align_bytes=64)
             nc.vector.quantize_mx(out=codes[:].bitcast(FP8X4), scales=scales[:],
-                                  in_=live["g", e][us[0] if n == 1 else 2])
+                                  in_=live["g", e][:, us[0]:us[-1] + 1, :].rearrange("p u k -> p (u k)"))
             cols = slice(e * C, (e + 1) * C)
             for i, u in enumerate(us):
                 acc = psum.tile([P, 4, C], F32, name=f"acc{u}", bufs=2)
@@ -115,55 +118,50 @@ def tile_routed_moe_kernel(tc, xT, w1, w3, w2, gate, offs, pos1, pos2, out):
                 live["acc", u, e] = acc
 
         def silu(e):
-            after = f"w_raw0_{LAST}" if e == LAST - 1 else f"w_raw1_{min(e + 1, LAST)}"
-            sil = held.tile([P, C, 4], F32, name=f"sil{e}", tag=after, align_bytes=DMA_ALIGN)
-            nc.scalar.activation(sil[:], live["acc", 0, e][:].rearrange("p t c -> p c t"), SILU)
+            if e in SHARED:
+                start = ahead.get((1, e), 0) + ROW - LAP
+                sil = w_tile[1, e][:, start:start + 4 * C].rearrange("p (c t) -> p c t", t=4)
+            else:
+                ring = stage.tile([P, C, 4], F32, name="sil", align_bytes=64)
+                sil = ring[:]
+            nc.scalar.activation(sil, live["acc", 0, e][:].rearrange("p t c -> p c t"), SILU)
             live["sil", e] = sil
 
-        def inter2(g):
-            grouped = held.tile([P, len(g), N * J], BF16, name=f"grp2_{g[0]}", align_bytes=64)
-            src = w2_raw[g][:].rearrange("p e (j c i) -> p e c j i", j=J, i=4)
-            dst = grouped[:].rearrange("p e (c i j) -> p e c j i", i=4, j=J)
-            cut = len(g) - (g[-1] in W2_ON_VECTOR)
-            if cut:
-                nc.scalar.copy(out=dst[:, 0:cut], in_=src[:, 0:cut])
-            if cut < len(g):
-                nc.vector.tensor_copy(out=dst[:, cut], in_=src[:, cut])
-            live["g2", g] = grouped
+        def hidden(e):
+            nc.vector.tensor_tensor(h_of[e].rearrange("p (c t) -> p c t", t=4), live["acc", 1, e][:].rearrange("p t c -> p c t"), live["sil", e], MULT)
 
-        def quant2(g):
-            codes = held.tile([P, len(g), N], U32, name=f"cod2_{g[0]}", align_bytes=64)
-            scales = held.tile([P, len(g), N], U8, name=f"scl2_{g[0]}", align_bytes=64)
-            nc.vector.quantize_mx(
-                out=codes[:].rearrange("p e n -> p (e n)").bitcast(FP8X4),
-                scales=scales[:].rearrange("p e n -> p (e n)"), in_=live["g2", g][:].rearrange("p e n -> p (e n)"))
-            for i, e in enumerate(g):
-                live["w2", e] = codes[:, i, :], scales[:, i, :]
-
-        h_group_of = {e: g for g in H_GROUPS for e in g}
-
-        def hid(e):
-            grp = h_group_of[e]
-            if e == grp[0]:
-                if grp[-1] == LAST - 1:
-                    live["hb", grp] = last_stage[:, H * J:H * J + 8 * C].rearrange("p (e c t) -> p e c t", e=2, t=4)
-                else:
-                    hb = stage.tile([P, 2, C, 4], BF16, name="hb", align_bytes=64)
-                    live["hb", grp] = hb[:]
-            nc.vector.tensor_tensor(live["hb", grp][:, e - grp[0]], live["acc", 1, e][:].rearrange("p t c -> p c t"), live["sil", e][:], MULT)
-
-        def quanth(grp):
-            n = len(grp)
-            codes = held.tile([P, n, C], U32, name=f"codh{grp[0]}", align_bytes=64)
-            scales = held.tile([P, n, C], U8, name=f"sclh{grp[0]}", align_bytes=64)
+        def quant_pieces(names, values):
+            n = len(names)
+            codes = held.tile([P, n, C], U32, name=f"codes_{names[0][0]}{names[0][1]}", align_bytes=64)
+            scales = held.tile([P, n, C], U8, name=f"scales_{names[0][0]}{names[0][1]}", align_bytes=64)
             nc.vector.quantize_mx(out=codes[:].rearrange("p e c -> p (e c)").bitcast(FP8X4),
-                                  scales=scales[:].rearrange("p e c -> p (e c)"),
-                                  in_=live["hb", grp][:, 0:n].rearrange("p e c t -> p (e c t)"))
-            for i, e in enumerate(grp):
-                live["qh", e] = codes[:, i, :], scales[:, i, :]
+                                  scales=scales[:].rearrange("p e c -> p (e c)"), in_=values)
+            for i, name in enumerate(names):
+                live[name] = codes[:, i, :], scales[:, i, :]
 
-        def down(grp):
-            acc = psum.tile([P, len(grp), C], F32, name=f"acc_y{grp[0]}")
+        w2_staged = held.tile([P, E, N * J], BF16, name="w2_staged", tag="w_raw0_3", align_bytes=DMA_ALIGN)
+        load_of = {e: g for g in W2_LOADS for e in g}
+
+        def round_w2(first, count):
+            g = load_of[first]
+            src = w2_raw[g][:, first - g[0]:first - g[0] + count].rearrange("p e (j c i) -> p e c j i", j=J, i=4)
+            staged = late[:, 0:N * J].unsqueeze(1) if first == 5 else w2_staged[:, first:first + count]
+            dst = staged.rearrange("p e (c i j) -> p e c j i", i=4, j=J)
+            copy = nc.vector.tensor_copy if first in W2_ON_VECTOR else nc.scalar.copy
+            if count == 1:
+                copy(out=dst[:, 0], in_=src[:, 0])
+            else:
+                copy(out=dst, in_=src)
+
+        def quant_w2(first, count):
+            quant_pieces([("w2", e) for e in range(first, first + count)],
+                         w2_staged[:, first:first + count].rearrange("p e n -> p (e n)"))
+
+        def second_layer(grp):
+            if grp[0] == 0:
+                acc = psum.tile([P, 4, C], F32, name="acc_y0", tag="acc0", bufs=2)
+            else:
+                acc = psum.tile([P, 4, C], F32, name=f"acc_y{grp[0]}")
             for i, e in enumerate(grp):
                 codes, scales = live["qh", e]
                 w2c, w2s = live["w2", e]
@@ -171,38 +169,55 @@ def tile_routed_moe_kernel(tc, xT, w1, w3, w2, gate, offs, pos1, pos2, out):
                     out=acc[:, i, :], lhsT=w2c.bitcast(FP8X4), lhsT_scale=w2s,
                     rhs=codes.bitcast(FP8X4), rhs_scale=scales, start=True, stop=True)
             copy = nc.vector.tensor_copy if grp[-1] == LAST else nc.scalar.copy
-            copy(out=y_sb[:, grp[0] * C:(grp[-1] + 1) * C], in_=acc[:].rearrange("p e c -> p (e c)"))
+            copy(out=y_sb[:, grp[0] * C:(grp[-1] + 1) * C], in_=acc[:, 0:len(grp), :].rearrange("p e c -> p (e c)"))
 
-        for e in range(E):
+        for e in range(SHARED[0]):
             if e in GATHERS:
                 gather(*GATHERS[e])
-            inter(0, e, LAST_W1_ON_SCALAR if e == LAST else P)
-            if e == LAST:
-                quant((0,), e)
+            round_w(0, e, P)
+            if e:
                 silu(e - 1)
-            inter(1, e, W3_ON_SCALAR.get(e, 0))
-            quant((0, 1) if e in JOINT else (1,), e)
-            if 0 < e < LAST:
-                silu(e - 1)
-                hid(e - 1)
-                if e - 1 == h_group_of[e - 1][-1]:
-                    quanth(h_group_of[e - 1])
+            round_w(1, e, 0)
+            if e:
+                hidden(e - 1)
+            first_layer((0, 1), e)
+            if e in (2, 4):
+                quant_pieces([("qh", e - 2), ("qh", e - 1)], h_early[:, e - 2:e].rearrange("p e n -> p (e n)"))
+        e = LAST - 1
+        round_w(0, e, ON_SCALAR[0])
+        first_layer((0,), e)
+        silu(e - 1)
+        round_w(1, e, ON_SCALAR[1])
+        hidden(e - 1)
+        first_layer((1,), e)
+        silu(e)
+        quant_pieces([("qh", e - 2), ("qh", e - 1)], h_mid)
+        round_w(0, LAST, ON_SCALAR[0])
+        hidden(e)
+        first_layer((0,), LAST)
+        round_w(1, LAST, ON_SCALAR[1])
+        first_layer((1,), LAST)
         silu(LAST)
-        hid(LAST - 1)
-        hid(LAST)
-        quanth(H_GROUPS[-2])
-        quanth(H_GROUPS[-1])
-        for grp in W2_LOADS:
-            inter2(grp)
-            quant2(grp)
+        round_w2(0, 2)
+        quant_w2(0, 2)
+        hidden(LAST)
+        round_w2(2, 2)
+        round_w2(4, 1)
+        round_w2(5, 1)
+        quant_w2(2, 2)
+        quant_pieces([("w2", 5), ("qh", LAST), ("qh", LAST - 1)], late)
+        quant_w2(4, 1)
+        round_w2(6, 1)
+        round_w2(7, 1)
+        quant_w2(6, 1)
+        quant_w2(7, 1)
         y_sb = held.tile([P, SLOTS], F32, name="y_sb", tag=f"w2_raw{W2_LOADS[-2][0]}", align_bytes=DMA_ALIGN)
-        for grp in ((0, 1, 2, 3), (4, 5), (6,), (7,)):
-            down(grp)
+        for grp in W2_LOADS:
+            second_layer(grp)
 
         r1 = held.tile([P, T], F32, name="r1", tag="x_raw", align_bytes=DMA_ALIGN)
         r2 = held.tile([P, T], F32, name="r2", tag="w_raw0_0", align_bytes=DMA_ALIGN)
         res = held.tile([P, T], F32, name="res", tag="w_raw0_1", align_bytes=DMA_ALIGN)
-
         p2 = held.tile([P, T], F32, name="p2", tag="w_raw0_2", align_bytes=DMA_ALIGN)
         parts = slice(0, FIRST_PART), slice(FIRST_PART, T)
         nc.vector.tensor_tensor(r1[:], y_sb[:].indirect(pos1_t[:]), gates[0][:], MULT)

@@ -23,14 +23,15 @@ DMA_ALIGN = 256
 LAST = E - 1
 W2_LOADS = ((0, 1), (2, 3), (4, 5), (6,), (7,))
 W2_ON_VECTOR = (0, 1, 5, 7)
-SHARED = (E - 2, E - 1)
 ROW = J * H
-LAP = 16
+LAP = 32
 PIECE = C * 4 // 2
+LEAD = 16
 FIRST_PART = 256
 GATHERS = {0: (0, 2), 1: (2, 3), 2: (5, 3)}
 X_ON_VECTOR = 344
-ON_SCALAR = (64, 48)
+W3_ON_SCALAR = {E - 2: 32, E - 1: 44}
+LAST_W1_ON_SCALAR = 64
 
 
 def tile_routed_moe_kernel(tc, xT, w1, w3, w2, gate, offs, pos1, pos2, out):
@@ -45,11 +46,16 @@ def tile_routed_moe_kernel(tc, xT, w1, w3, w2, gate, offs, pos1, pos2, out):
         pos2_t = held.tile([P, T // 16], U16, name="pos2_t")
         x_raw = held.tile([P, J, T], F32, name="x_raw", align_bytes=DMA_ALIGN)
         gates = [held.tile([P, T], F32, name=f"gate{g}", align_bytes=DMA_ALIGN) for g in range(2)]
-        ahead = {(1, LAST - 1): 2 * PIECE, (0, LAST): 3 * PIECE}
-        behind = {(1, LAST - 1): 2 * PIECE, (1, LAST): 2 * PIECE}
-        w_tile = {(u, e): held.tile([P, ahead.get((u, e), 0) + ROW + behind.get((u, e), 0)], F32, name=f"w_raw{u}_{e}", align_bytes=DMA_ALIGN)
-                  for e in range(E) for u in range(2)}
-        w_raw = {k: t[:, ahead.get(k, 0):ahead.get(k, 0) + ROW] for k, t in w_tile.items()}
+        w_raw = {}
+        for e in range(LAST):
+            for u in range(2):
+                raw = held.tile([P, ROW], F32, name=f"w_raw{u}_{e}", align_bytes=DMA_ALIGN)
+                w_raw[u, e] = raw[:]
+        first_at = 2 * PIECE
+        second_at = first_at + ROW + 2 * PIECE - 2 * LAP
+        last_raw = held.tile([P, second_at + ROW + 2 * PIECE], F32, name="last_raw", align_bytes=DMA_ALIGN)
+        w_raw[0, LAST] = last_raw[:, first_at:first_at + ROW]
+        w_raw[1, LAST] = last_raw[:, second_at:second_at + ROW]
         w2_raw = {g: held.tile([P, len(g), J * N], F32, name=f"w2_raw{g[0]}", align_bytes=DMA_ALIGN) for g in W2_LOADS}
 
         nc.sync.dma_start(out=x_raw[:], in_=xT.rearrange("(p j) t -> p j t", j=J))
@@ -76,12 +82,12 @@ def tile_routed_moe_kernel(tc, xT, w1, w3, w2, gate, offs, pos1, pos2, out):
 
         s_codes = held.tile([P, SLOTS], U32, name="s_codes", align_bytes=64)
         s_scales = held.tile([P, SLOTS], U8, name="s_scales", align_bytes=64)
-        h_early = held.tile([P, 4, C * 4], BF16, name="h_early", align_bytes=64)
-        h_mid = w_tile[1, LAST - 1][:, LAP:LAP + 2 * PIECE].bitcast(BF16)
-        late = w_tile[0, LAST][:, LAP:LAP + 3 * PIECE].bitcast(BF16)
-        h_of = {e: h_early[:, e, :] for e in range(4)}
-        h_of[4], h_of[5] = h_mid[:, 0:4 * C], h_mid[:, 4 * C:]
-        h_of[LAST], h_of[LAST - 1] = late[:, 4 * C:8 * C], late[:, 8 * C:]
+        h_early = held.tile([P, LAST - 2, C * 4], BF16, name="h_early", align_bytes=64)
+        h_pair = last_raw[:, first_at + ROW - LAP:second_at + LAP].bitcast(BF16)
+        late = held.tile([P, 3, C * 4], BF16, name="late", align_bytes=64)
+        h_of = {e: h_early[:, e, :] for e in range(LAST - 2)}
+        h_of[LAST - 2], h_of[LAST - 1], h_of[LAST] = h_pair[:, 0:4 * C], h_pair[:, 4 * C:], late[:, 2, :]
+        sil_at = {LAST - 1: LAP, LAST: second_at + ROW - LAP}
         live = {}
 
         def gather(first, count):
@@ -90,16 +96,15 @@ def tile_routed_moe_kernel(tc, xT, w1, w3, w2, gate, offs, pos1, pos2, out):
             nc.vector.tensor_copy(s_codes[:, cols], x_codes[:].indirect(lst))
             nc.vector.tensor_copy(s_scales[:, cols], x_scales[:].indirect(lst))
 
-        def round_w(u, e, on_scalar):
+        def round_w(u, e, on_vector, on_scalar):
             if u == 0:
                 live["g", e] = stage.tile([P, 2, H * J], BF16, name="grouped", align_bytes=64)
             src = w_raw[u, e].rearrange("p (j m t) -> p m j t", j=J, t=4)
             dst = live["g", e][:, u, :].rearrange("p (t m j) -> p m j t", t=4, j=J)
-            cut = P - on_scalar
-            if cut:
-                nc.vector.tensor_copy(out=dst[:, 0:cut], in_=src[:, 0:cut])
-            if on_scalar:
-                nc.scalar.copy(out=dst[:, cut:], in_=src[:, cut:])
+            for part in on_vector:
+                nc.vector.tensor_copy(out=dst[:, part], in_=src[:, part])
+            for part in on_scalar:
+                nc.scalar.copy(out=dst[:, part], in_=src[:, part])
 
         def first_layer(us, e):
             n = len(us)
@@ -118,12 +123,11 @@ def tile_routed_moe_kernel(tc, xT, w1, w3, w2, gate, offs, pos1, pos2, out):
                 live["acc", u, e] = acc
 
         def silu(e):
-            if e in SHARED:
-                start = ahead.get((1, e), 0) + ROW - LAP
-                sil = w_tile[1, e][:, start:start + 4 * C].rearrange("p (c t) -> p c t", t=4)
+            if e in sil_at:
+                sil = last_raw[:, sil_at[e]:sil_at[e] + 4 * C].rearrange("p (c t) -> p c t", t=4)
             else:
-                ring = stage.tile([P, C, 4], F32, name="sil", align_bytes=64)
-                sil = ring[:]
+                own = held.tile([P, C, 4], F32, name=f"sil{e}", tag=f"w_raw1_{e + 1}", align_bytes=DMA_ALIGN)
+                sil = own[:]
             nc.scalar.activation(sil, live["acc", 0, e][:].rearrange("p t c -> p c t"), SILU)
             live["sil", e] = sil
 
@@ -145,7 +149,7 @@ def tile_routed_moe_kernel(tc, xT, w1, w3, w2, gate, offs, pos1, pos2, out):
         def round_w2(first, count):
             g = load_of[first]
             src = w2_raw[g][:, first - g[0]:first - g[0] + count].rearrange("p e (j c i) -> p e c j i", j=J, i=4)
-            staged = late[:, 0:N * J].unsqueeze(1) if first == 5 else w2_staged[:, first:first + count]
+            staged = late[:, first - 4:first - 3] if first in (4, 5) else w2_staged[:, first:first + count]
             dst = staged.rearrange("p e (c i j) -> p e c j i", i=4, j=J)
             copy = nc.vector.tensor_copy if first in W2_ON_VECTOR else nc.scalar.copy
             if count == 1:
@@ -171,42 +175,38 @@ def tile_routed_moe_kernel(tc, xT, w1, w3, w2, gate, offs, pos1, pos2, out):
             copy = nc.vector.tensor_copy if grp[-1] == LAST else nc.scalar.copy
             copy(out=y_sb[:, grp[0] * C:(grp[-1] + 1) * C], in_=acc[:, 0:len(grp), :].rearrange("p e c -> p (e c)"))
 
-        for e in range(SHARED[0]):
+        for e in range(LAST):
             if e in GATHERS:
                 gather(*GATHERS[e])
-            round_w(0, e, P)
+            round_w(0, e, [], [slice(0, P)])
+            cut = P - W3_ON_SCALAR.get(e, 0)
+            round_w(1, e, [slice(0, cut)], [slice(cut, P)] if cut < P else [])
+            first_layer((0, 1), e)
             if e:
                 silu(e - 1)
-            round_w(1, e, 0)
-            if e:
+            if 0 < e < LAST - 1:
                 hidden(e - 1)
-            first_layer((0, 1), e)
-            if e in (2, 4):
-                quant_pieces([("qh", e - 2), ("qh", e - 1)], h_early[:, e - 2:e].rearrange("p e n -> p (e n)"))
-        e = LAST - 1
-        round_w(0, e, ON_SCALAR[0])
-        first_layer((0,), e)
-        silu(e - 1)
-        round_w(1, e, ON_SCALAR[1])
-        hidden(e - 1)
-        first_layer((1,), e)
-        silu(e)
-        quant_pieces([("qh", e - 2), ("qh", e - 1)], h_mid)
-        round_w(0, LAST, ON_SCALAR[0])
-        hidden(e)
+            if e in (1, 3, 5):
+                group = range(max(e - 2, 0), e)
+                quant_pieces([("qh", i) for i in group], h_early[:, group.start:group.stop].rearrange("p e n -> p (e n)"))
+        round_w(0, LAST, [slice(P - LEAD, P), slice(LAST_W1_ON_SCALAR, P - LEAD)], [slice(0, LAST_W1_ON_SCALAR)])
+        hidden(LAST - 2)
         first_layer((0,), LAST)
-        round_w(1, LAST, ON_SCALAR[1])
+        silu(LAST - 1)
+        cut = P - W3_ON_SCALAR[LAST]
+        round_w(1, LAST, [slice(0, LEAD), slice(LEAD, cut)], [slice(cut, P)])
+        hidden(LAST - 1)
         first_layer((1,), LAST)
         silu(LAST)
         round_w2(0, 2)
+        quant_pieces([("qh", LAST - 2), ("qh", LAST - 1)], h_pair)
         quant_w2(0, 2)
         hidden(LAST)
         round_w2(2, 2)
         round_w2(4, 1)
         round_w2(5, 1)
         quant_w2(2, 2)
-        quant_pieces([("w2", 5), ("qh", LAST), ("qh", LAST - 1)], late)
-        quant_w2(4, 1)
+        quant_pieces([("w2", 4), ("w2", 5), ("qh", LAST)], late[:].rearrange("p e n -> p (e n)"))
         round_w2(6, 1)
         round_w2(7, 1)
         quant_w2(6, 1)

@@ -26,12 +26,10 @@ W2_ON_VECTOR = (0, 1, 5, 7)
 ROW = J * H
 LAP = 32
 PIECE = C * 4 // 2
-LEAD = 16
 FIRST_PART = 256
 GATHERS = {0: (0, 2), 1: (2, 3), 2: (5, 3)}
 X_ON_VECTOR = 344
-W3_ON_SCALAR = {E - 2: 32, E - 1: 44}
-LAST_W1_ON_SCALAR = 64
+ON_SCALAR = {(0, E - 2): 80, (1, E - 2): 40, (0, E - 1): 56, (1, E - 1): 44}
 
 
 def tile_routed_moe_kernel(tc, xT, w1, w3, w2, gate, offs, pos1, pos2, out):
@@ -45,17 +43,12 @@ def tile_routed_moe_kernel(tc, xT, w1, w3, w2, gate, offs, pos1, pos2, out):
         pos1_t = held.tile([P, T // 16], U16, name="pos1_t")
         pos2_t = held.tile([P, T // 16], U16, name="pos2_t")
         x_raw = held.tile([P, J, T], F32, name="x_raw", align_bytes=DMA_ALIGN)
-        gates = [held.tile([P, T], F32, name=f"gate{g}", align_bytes=DMA_ALIGN) for g in range(2)]
-        w_raw = {}
-        for e in range(LAST):
-            for u in range(2):
-                raw = held.tile([P, ROW], F32, name=f"w_raw{u}_{e}", align_bytes=DMA_ALIGN)
-                w_raw[u, e] = raw[:]
-        first_at = 2 * PIECE
-        second_at = first_at + ROW + 2 * PIECE - 2 * LAP
-        last_raw = held.tile([P, second_at + ROW + 2 * PIECE], F32, name="last_raw", align_bytes=DMA_ALIGN)
-        w_raw[0, LAST] = last_raw[:, first_at:first_at + ROW]
-        w_raw[1, LAST] = last_raw[:, second_at:second_at + ROW]
+        gates = held.tile([P, 2, T], F32, name="gates", align_bytes=DMA_ALIGN)
+        ahead = {(1, LAST): PIECE}
+        behind = {(1, LAST - 1): 2 * PIECE, (1, LAST): 2 * PIECE}
+        w_tile = {(u, e): held.tile([P, ahead.get((u, e), 0) + ROW + behind.get((u, e), 0)], F32, name=f"w_raw{u}_{e}", align_bytes=DMA_ALIGN)
+                  for e in range(E) for u in range(2)}
+        w_raw = {k: t[:, ahead.get(k, 0):ahead.get(k, 0) + ROW] for k, t in w_tile.items()}
         w2_raw = {g: held.tile([P, len(g), J * N], F32, name=f"w2_raw{g[0]}", align_bytes=DMA_ALIGN) for g in W2_LOADS}
 
         nc.sync.dma_start(out=x_raw[:], in_=xT.rearrange("(p j) t -> p j t", j=J))
@@ -65,9 +58,9 @@ def tile_routed_moe_kernel(tc, xT, w1, w3, w2, gate, offs, pos1, pos2, out):
                 nc.sync.dma_start(out=w_raw[u, e], in_=w[e, :, :].rearrange("(p j) h -> p (j h)", j=J))
         for g in W2_LOADS:
             nc.sync.dma_start(out=w2_raw[g][:], in_=w2[g[0]:g[-1] + 1, :, :].rearrange("e (p j) n -> p e (j n)", j=J))
-        for lst, pos, g in ((pos1_t, pos1, 0), (pos2_t, pos2, 1)):
-            nc.sync.dma_start(lst[:], pos)
-            nc.sync.dma_start(out=gates[g][:], in_=gate[g, :, :])
+        nc.sync.dma_start(pos1_t[:], pos1)
+        nc.sync.dma_start(pos2_t[:], pos2)
+        nc.sync.dma_start(out=gates[:], in_=gate.rearrange("g n t -> n g t"))
 
         x_codes = held.tile([P, T], U32, name="x_codes", align_bytes=64)
         x_scales = held.tile([P, T], U8, name="x_scales", align_bytes=64)
@@ -83,11 +76,11 @@ def tile_routed_moe_kernel(tc, xT, w1, w3, w2, gate, offs, pos1, pos2, out):
         s_codes = held.tile([P, SLOTS], U32, name="s_codes", align_bytes=64)
         s_scales = held.tile([P, SLOTS], U8, name="s_scales", align_bytes=64)
         h_early = held.tile([P, LAST - 2, C * 4], BF16, name="h_early", align_bytes=64)
-        h_pair = last_raw[:, first_at + ROW - LAP:second_at + LAP].bitcast(BF16)
-        late = held.tile([P, 3, C * 4], BF16, name="late", align_bytes=64)
+        h_pair = w_tile[1, LAST][:, 0:2 * PIECE].bitcast(BF16)
+        late = held.tile([P, 2, C * 4], BF16, name="late", align_bytes=64)
         h_of = {e: h_early[:, e, :] for e in range(LAST - 2)}
-        h_of[LAST - 2], h_of[LAST - 1], h_of[LAST] = h_pair[:, 0:4 * C], h_pair[:, 4 * C:], late[:, 2, :]
-        sil_at = {LAST - 1: LAP, LAST: second_at + ROW - LAP}
+        h_of[LAST - 2], h_of[LAST - 1], h_of[LAST] = h_pair[:, 0:4 * C], h_pair[:, 4 * C:], late[:, 1, :]
+        sil_behind = {LAST - 2: (1, LAST - 1), LAST: (1, LAST)}
         live = {}
 
         def gather(first, count):
@@ -113,8 +106,11 @@ def tile_routed_moe_kernel(tc, xT, w1, w3, w2, gate, offs, pos1, pos2, out):
             nc.vector.quantize_mx(out=codes[:].bitcast(FP8X4), scales=scales[:],
                                   in_=live["g", e][:, us[0]:us[-1] + 1, :].rearrange("p u k -> p (u k)"))
             cols = slice(e * C, (e + 1) * C)
-            for i, u in enumerate(us):
-                acc = psum.tile([P, 4, C], F32, name=f"acc{u}", bufs=2)
+            for i, u in reversed(list(enumerate(us))):
+                if (u, e) == (1, LAST):
+                    acc = live["acc", 0, e]
+                else:
+                    acc = psum.tile([P, 4, C], F32, name=f"acc{u}", bufs=2)
                 for t in range(4):
                     blk = slice(i * H + t * P, i * H + (t + 1) * P)
                     nc.tensor.matmul_mx(
@@ -123,10 +119,12 @@ def tile_routed_moe_kernel(tc, xT, w1, w3, w2, gate, offs, pos1, pos2, out):
                 live["acc", u, e] = acc
 
         def silu(e):
-            if e in sil_at:
-                sil = last_raw[:, sil_at[e]:sil_at[e] + 4 * C].rearrange("p (c t) -> p c t", t=4)
+            if e in sil_behind:
+                start = ahead.get(sil_behind[e], 0) + ROW - LAP
+                sil = w_tile[sil_behind[e]][:, start:start + 4 * C].rearrange("p (c t) -> p c t", t=4)
             else:
-                own = held.tile([P, C, 4], F32, name=f"sil{e}", tag=f"w_raw1_{e + 1}", align_bytes=DMA_ALIGN)
+                tag = f"w_raw1_{e + 1}" if e < LAST - 2 else "w_raw0_4"
+                own = held.tile([P, C, 4], F32, name=f"sil{e}", tag=tag, align_bytes=DMA_ALIGN)
                 sil = own[:]
             nc.scalar.activation(sil, live["acc", 0, e][:].rearrange("p t c -> p c t"), SILU)
             live["sil", e] = sil
@@ -143,13 +141,16 @@ def tile_routed_moe_kernel(tc, xT, w1, w3, w2, gate, offs, pos1, pos2, out):
             for i, name in enumerate(names):
                 live[name] = codes[:, i, :], scales[:, i, :]
 
+        def quant_h_early(group):
+            quant_pieces([("qh", i) for i in group], h_early[:, group.start:group.stop].rearrange("p e n -> p (e n)"))
+
         w2_staged = held.tile([P, E, N * J], BF16, name="w2_staged", tag="w_raw0_3", align_bytes=DMA_ALIGN)
         load_of = {e: g for g in W2_LOADS for e in g}
 
         def round_w2(first, count):
             g = load_of[first]
             src = w2_raw[g][:, first - g[0]:first - g[0] + count].rearrange("p e (j c i) -> p e c j i", j=J, i=4)
-            staged = late[:, first - 4:first - 3] if first in (4, 5) else w2_staged[:, first:first + count]
+            staged = late[:, 0:1] if first == 5 else w2_staged[:, first:first + count]
             dst = staged.rearrange("p e (c i j) -> p e c j i", i=4, j=J)
             copy = nc.vector.tensor_copy if first in W2_ON_VECTOR else nc.scalar.copy
             if count == 1:
@@ -172,32 +173,40 @@ def tile_routed_moe_kernel(tc, xT, w1, w3, w2, gate, offs, pos1, pos2, out):
                 nc.tensor.matmul_mx(
                     out=acc[:, i, :], lhsT=w2c.bitcast(FP8X4), lhsT_scale=w2s,
                     rhs=codes.bitcast(FP8X4), rhs_scale=scales, start=True, stop=True)
-            copy = nc.vector.tensor_copy if grp[-1] == LAST else nc.scalar.copy
-            copy(out=y_sb[:, grp[0] * C:(grp[-1] + 1) * C], in_=acc[:, 0:len(grp), :].rearrange("p e c -> p (e c)"))
+            nc.scalar.copy(out=y_sb[:, grp[0] * C:(grp[-1] + 1) * C], in_=acc[:, 0:len(grp), :].rearrange("p e c -> p (e c)"))
 
-        for e in range(LAST):
+        for e in range(LAST - 1):
             if e in GATHERS:
                 gather(*GATHERS[e])
             round_w(0, e, [], [slice(0, P)])
-            cut = P - W3_ON_SCALAR.get(e, 0)
-            round_w(1, e, [slice(0, cut)], [slice(cut, P)] if cut < P else [])
+            round_w(1, e, [slice(0, P)], [])
             first_layer((0, 1), e)
             if e:
                 silu(e - 1)
-            if 0 < e < LAST - 1:
                 hidden(e - 1)
-            if e in (1, 3, 5):
-                group = range(max(e - 2, 0), e)
-                quant_pieces([("qh", i) for i in group], h_early[:, group.start:group.stop].rearrange("p e n -> p (e n)"))
-        round_w(0, LAST, [slice(P - LEAD, P), slice(LAST_W1_ON_SCALAR, P - LEAD)], [slice(0, LAST_W1_ON_SCALAR)])
-        hidden(LAST - 2)
+            if e in (1, 3):
+                quant_h_early(range(max(e - 2, 0), e))
+
+        def shared(u, e):
+            n = ON_SCALAR[u, e]
+            low, high = (slice(0, n), slice(n, P)) if (u, e) == (1, LAST) else (slice(P - n, P), slice(0, P - n))
+            round_w(u, e, [high], [low])
+
+        e = LAST - 1
+        shared(0, e)
+        quant_h_early(range(e - 3, e - 1))
+        first_layer((0,), e)
+        shared(1, e)
+        first_layer((1,), e)
+        silu(e - 1)
+        hidden(e - 1)
+        silu(e)
+        shared(0, LAST)
         first_layer((0,), LAST)
-        silu(LAST - 1)
-        cut = P - W3_ON_SCALAR[LAST]
-        round_w(1, LAST, [slice(0, LEAD), slice(LEAD, cut)], [slice(cut, P)])
-        hidden(LAST - 1)
-        first_layer((1,), LAST)
+        shared(1, LAST)
         silu(LAST)
+        first_layer((1,), LAST)
+        hidden(e)
         round_w2(0, 2)
         quant_pieces([("qh", LAST - 2), ("qh", LAST - 1)], h_pair)
         quant_w2(0, 2)
@@ -206,7 +215,8 @@ def tile_routed_moe_kernel(tc, xT, w1, w3, w2, gate, offs, pos1, pos2, out):
         round_w2(4, 1)
         round_w2(5, 1)
         quant_w2(2, 2)
-        quant_pieces([("w2", 4), ("w2", 5), ("qh", LAST)], late[:].rearrange("p e n -> p (e n)"))
+        quant_pieces([("w2", 5), ("qh", LAST)], late[:].rearrange("p e n -> p (e n)"))
+        quant_w2(4, 1)
         round_w2(6, 1)
         round_w2(7, 1)
         quant_w2(6, 1)
@@ -220,11 +230,11 @@ def tile_routed_moe_kernel(tc, xT, w1, w3, w2, gate, offs, pos1, pos2, out):
         res = held.tile([P, T], F32, name="res", tag="w_raw0_1", align_bytes=DMA_ALIGN)
         p2 = held.tile([P, T], F32, name="p2", tag="w_raw0_2", align_bytes=DMA_ALIGN)
         parts = slice(0, FIRST_PART), slice(FIRST_PART, T)
-        nc.vector.tensor_tensor(r1[:], y_sb[:].indirect(pos1_t[:]), gates[0][:], MULT)
+        nc.vector.tensor_tensor(r1[:], y_sb[:].indirect(pos1_t[:]), gates[:, 0, :], MULT)
         for toks in parts:
             nc.scalar.activation(r2[:, toks], y_sb[:].indirect(pos2_t[:, toks.start // 16:toks.stop // 16]), COPY)
         for toks in parts:
-            nc.vector.tensor_tensor(p2[:, toks], r2[:, toks], gates[1][:, toks], MULT)
+            nc.vector.tensor_tensor(p2[:, toks], r2[:, toks], gates[:, 1, toks], MULT)
         for queue, toks in zip((nc.sync, nc.scalar), parts):
             nc.vector.tensor_tensor(res[:, toks], r1[:, toks], p2[:, toks], ADD)
             queue.dma_start(out=out[:, toks], in_=res[:, toks])

@@ -22,14 +22,14 @@ J = 4
 DMA_ALIGN = 256
 LAST = E - 1
 W2_LOADS = ((0, 1), (2, 3), (4, 5), (6,), (7,))
-W2_ON_VECTOR = (0, 1, 5, 7)
+W2_ON_VECTOR = (1, 5, 7)
 ROW = J * H
 LAP = 32
 PIECE = C * 4 // 2
 FIRST_PART = 256
 GATHERS = {0: (0, 2), 1: (2, 3), 2: (5, 3)}
 X_ON_VECTOR = 344
-ON_SCALAR = {(0, E - 2): 80, (1, E - 2): 40, (0, E - 1): 56, (1, E - 1): 44}
+ON_SCALAR = {(1, E - 2): 40, (0, E - 1): 80, (1, E - 1): 50}
 
 
 def tile_routed_moe_kernel(tc, xT, w1, w3, w2, gate, offs, pos1, pos2, out):
@@ -44,8 +44,8 @@ def tile_routed_moe_kernel(tc, xT, w1, w3, w2, gate, offs, pos1, pos2, out):
         pos2_t = held.tile([P, T // 16], U16, name="pos2_t")
         x_raw = held.tile([P, J, T], F32, name="x_raw", align_bytes=DMA_ALIGN)
         gates = held.tile([P, 2, T], F32, name="gates", align_bytes=DMA_ALIGN)
-        ahead = {(1, LAST): PIECE}
-        behind = {(1, LAST - 1): 2 * PIECE, (1, LAST): 2 * PIECE}
+        ahead = {(1, LAST): 2 * PIECE}
+        behind = {(1, LAST): 2 * PIECE}
         w_tile = {(u, e): held.tile([P, ahead.get((u, e), 0) + ROW + behind.get((u, e), 0)], F32, name=f"w_raw{u}_{e}", align_bytes=DMA_ALIGN)
                   for e in range(E) for u in range(2)}
         w_raw = {k: t[:, ahead.get(k, 0):ahead.get(k, 0) + ROW] for k, t in w_tile.items()}
@@ -58,9 +58,9 @@ def tile_routed_moe_kernel(tc, xT, w1, w3, w2, gate, offs, pos1, pos2, out):
                 nc.sync.dma_start(out=w_raw[u, e], in_=w[e, :, :].rearrange("(p j) h -> p (j h)", j=J))
         for g in W2_LOADS:
             nc.sync.dma_start(out=w2_raw[g][:], in_=w2[g[0]:g[-1] + 1, :, :].rearrange("e (p j) n -> p e (j n)", j=J))
-        nc.sync.dma_start(pos1_t[:], pos1)
-        nc.sync.dma_start(pos2_t[:], pos2)
-        nc.sync.dma_start(out=gates[:], in_=gate.rearrange("g n t -> n g t"))
+        for lst, pos, g in ((pos1_t, pos1, 0), (pos2_t, pos2, 1)):
+            nc.sync.dma_start(lst[:], pos)
+            nc.sync.dma_start(out=gates[:, g, :], in_=gate[g, :, :])
 
         x_codes = held.tile([P, T], U32, name="x_codes", align_bytes=64)
         x_scales = held.tile([P, T], U8, name="x_scales", align_bytes=64)
@@ -76,11 +76,11 @@ def tile_routed_moe_kernel(tc, xT, w1, w3, w2, gate, offs, pos1, pos2, out):
         s_codes = held.tile([P, SLOTS], U32, name="s_codes", align_bytes=64)
         s_scales = held.tile([P, SLOTS], U8, name="s_scales", align_bytes=64)
         h_early = held.tile([P, LAST - 2, C * 4], BF16, name="h_early", align_bytes=64)
-        h_pair = w_tile[1, LAST][:, 0:2 * PIECE].bitcast(BF16)
+        early = w_tile[1, LAST][:, 0:3 * PIECE].bitcast(BF16)
         late = held.tile([P, 2, C * 4], BF16, name="late", align_bytes=64)
         h_of = {e: h_early[:, e, :] for e in range(LAST - 2)}
-        h_of[LAST - 2], h_of[LAST - 1], h_of[LAST] = h_pair[:, 0:4 * C], h_pair[:, 4 * C:], late[:, 1, :]
-        sil_behind = {LAST - 2: (1, LAST - 1), LAST: (1, LAST)}
+        h_of[LAST - 2], h_of[LAST - 1], h_of[LAST] = early[:, 4 * C:8 * C], early[:, 8 * C:], late[:, 1, :]
+        sil_behind = {LAST: (1, LAST)}
         live = {}
 
         def gather(first, count):
@@ -106,11 +106,9 @@ def tile_routed_moe_kernel(tc, xT, w1, w3, w2, gate, offs, pos1, pos2, out):
             nc.vector.quantize_mx(out=codes[:].bitcast(FP8X4), scales=scales[:],
                                   in_=live["g", e][:, us[0]:us[-1] + 1, :].rearrange("p u k -> p (u k)"))
             cols = slice(e * C, (e + 1) * C)
-            for i, u in reversed(list(enumerate(us))):
-                if (u, e) == (1, LAST):
-                    acc = live["acc", 0, e]
-                else:
-                    acc = psum.tile([P, 4, C], F32, name=f"acc{u}", bufs=2)
+            order = list(enumerate(us))
+            for i, u in order if e == LAST - 1 else reversed(order):
+                acc = psum.tile([P, 4, C], F32, name=f"acc{u}", bufs=2)
                 for t in range(4):
                     blk = slice(i * H + t * P, i * H + (t + 1) * P)
                     nc.tensor.matmul_mx(
@@ -123,7 +121,7 @@ def tile_routed_moe_kernel(tc, xT, w1, w3, w2, gate, offs, pos1, pos2, out):
                 start = ahead.get(sil_behind[e], 0) + ROW - LAP
                 sil = w_tile[sil_behind[e]][:, start:start + 4 * C].rearrange("p (c t) -> p c t", t=4)
             else:
-                tag = f"w_raw1_{e + 1}" if e < LAST - 2 else "w_raw0_4"
+                tag = f"w_raw1_{e + 1}" if e < LAST - 1 else f"w_raw0_{LAST}"
                 own = held.tile([P, C, 4], F32, name=f"sil{e}", tag=tag, align_bytes=DMA_ALIGN)
                 sil = own[:]
             nc.scalar.activation(sil, live["acc", 0, e][:].rearrange("p t c -> p c t"), SILU)
@@ -150,7 +148,7 @@ def tile_routed_moe_kernel(tc, xT, w1, w3, w2, gate, offs, pos1, pos2, out):
         def round_w2(first, count):
             g = load_of[first]
             src = w2_raw[g][:, first - g[0]:first - g[0] + count].rearrange("p e (j c i) -> p e c j i", j=J, i=4)
-            staged = late[:, 0:1] if first == 5 else w2_staged[:, first:first + count]
+            staged = {1: early[:, 0:4 * C].unsqueeze(1), 5: late[:, 0:1]}.get(first, w2_staged[:, first:first + count])
             dst = staged.rearrange("p e (c i j) -> p e c j i", i=4, j=J)
             copy = nc.vector.tensor_copy if first in W2_ON_VECTOR else nc.scalar.copy
             if count == 1:
@@ -173,43 +171,39 @@ def tile_routed_moe_kernel(tc, xT, w1, w3, w2, gate, offs, pos1, pos2, out):
                 nc.tensor.matmul_mx(
                     out=acc[:, i, :], lhsT=w2c.bitcast(FP8X4), lhsT_scale=w2s,
                     rhs=codes.bitcast(FP8X4), rhs_scale=scales, start=True, stop=True)
-            nc.scalar.copy(out=y_sb[:, grp[0] * C:(grp[-1] + 1) * C], in_=acc[:, 0:len(grp), :].rearrange("p e c -> p (e c)"))
+            copy = nc.vector.tensor_copy if grp[-1] == LAST else nc.scalar.copy
+            copy(out=y_sb[:, grp[0] * C:(grp[-1] + 1) * C], in_=acc[:, 0:len(grp), :].rearrange("p e c -> p (e c)"))
 
-        for e in range(LAST - 1):
+        def shared(u, e):
+            n = ON_SCALAR[u, e]
+            on_scalar, on_vector = (slice(0, n), slice(n, P)) if (u, e) == (1, LAST) else (slice(P - n, P), slice(0, P - n))
+            round_w(u, e, [on_vector], [on_scalar])
+
+        for e in range(LAST):
             if e in GATHERS:
                 gather(*GATHERS[e])
             round_w(0, e, [], [slice(0, P)])
-            round_w(1, e, [slice(0, P)], [])
+            if (1, e) in ON_SCALAR:
+                shared(1, e)
+            else:
+                round_w(1, e, [slice(0, P)], [])
             first_layer((0, 1), e)
             if e:
                 silu(e - 1)
                 hidden(e - 1)
-            if e in (1, 3):
+            if e in (1, 3, 5):
                 quant_h_early(range(max(e - 2, 0), e))
-
-        def shared(u, e):
-            n = ON_SCALAR[u, e]
-            low, high = (slice(0, n), slice(n, P)) if (u, e) == (1, LAST) else (slice(P - n, P), slice(0, P - n))
-            round_w(u, e, [high], [low])
-
-        e = LAST - 1
-        shared(0, e)
-        quant_h_early(range(e - 3, e - 1))
-        first_layer((0,), e)
-        shared(1, e)
-        first_layer((1,), e)
-        silu(e - 1)
-        hidden(e - 1)
-        silu(e)
         shared(0, LAST)
         first_layer((0,), LAST)
+        silu(LAST - 1)
         shared(1, LAST)
-        silu(LAST)
         first_layer((1,), LAST)
-        hidden(e)
-        round_w2(0, 2)
-        quant_pieces([("qh", LAST - 2), ("qh", LAST - 1)], h_pair)
-        quant_w2(0, 2)
+        silu(LAST)
+        round_w2(0, 1)
+        round_w2(1, 1)
+        hidden(LAST - 1)
+        quant_w2(0, 1)
+        quant_pieces([("w2", 1), ("qh", LAST - 2), ("qh", LAST - 1)], early)
         hidden(LAST)
         round_w2(2, 2)
         round_w2(4, 1)

@@ -29,7 +29,7 @@ PIECE = C * 4 // 2
 FIRST_PART = 256
 GATHERS = {0: (0, 2), 1: (2, 3), 2: (5, 3)}
 X_ON_VECTOR = 344
-ON_SCALAR = {(1, E - 2): 40, (0, E - 1): 80, (1, E - 1): 50}
+ON_SCALAR = {(0, E - 2): 104, (1, E - 2): 48, (0, E - 1): 76, (1, E - 1): 50}
 
 
 def tile_routed_moe_kernel(tc, xT, w1, w3, w2, gate, offs, pos1, pos2, out):
@@ -182,7 +182,11 @@ def tile_routed_moe_kernel(tc, xT, w1, w3, w2, gate, offs, pos1, pos2, out):
         for e in range(LAST):
             if e in GATHERS:
                 gather(*GATHERS[e])
-            round_w(0, e, [], [slice(0, P)])
+            if (0, e) in ON_SCALAR:
+                shared(0, e)
+                quant_h_early(range(e - 3, e - 1))
+            else:
+                round_w(0, e, [], [slice(0, P)])
             if (1, e) in ON_SCALAR:
                 shared(1, e)
             else:
@@ -191,7 +195,7 @@ def tile_routed_moe_kernel(tc, xT, w1, w3, w2, gate, offs, pos1, pos2, out):
             if e:
                 silu(e - 1)
                 hidden(e - 1)
-            if e in (1, 3, 5):
+            if e in (1, 3):
                 quant_h_early(range(max(e - 2, 0), e))
         shared(0, LAST)
         first_layer((0,), LAST)
@@ -215,7 +219,7 @@ def tile_routed_moe_kernel(tc, xT, w1, w3, w2, gate, offs, pos1, pos2, out):
         round_w2(7, 1)
         quant_w2(6, 1)
         quant_w2(7, 1)
-        y_sb = held.tile([P, SLOTS], F32, name="y_sb", tag=f"w2_raw{W2_LOADS[-2][0]}", align_bytes=DMA_ALIGN)
+        y_sb = held.tile([P, SLOTS], F32, name="y_sb", tag=f"w2_raw{W2_LOADS[-3][0]}", align_bytes=DMA_ALIGN)
         for grp in W2_LOADS:
             second_layer(grp)
 

@@ -233,6 +233,6 @@ def tile_routed_moe_kernel(tc, xT, w1, w3, w2, gate, offs, pos1, pos2, out):
             nc.scalar.activation(r2[:, toks], y_sb[:].indirect(pos2_t[:, toks.start // 16:toks.stop // 16]), COPY)
         for toks in parts:
             nc.vector.tensor_tensor(p2[:, toks], r2[:, toks], gates[:, 1, toks], MULT)
-        for queue, toks in zip((nc.sync, nc.scalar), parts):
+        for toks in parts:
             nc.vector.tensor_tensor(res[:, toks], r1[:, toks], p2[:, toks], ADD)
-            queue.dma_start(out=out[:, toks], in_=res[:, toks])
+            nc.scalar.dma_start(out=out[:, toks], in_=res[:, toks])

@@ -171,7 +171,7 @@ def tile_routed_moe_kernel(tc, xT, w1, w3, w2, gate, offs, pos1, pos2, out):
                 nc.tensor.matmul_mx(
                     out=acc[:, i, :], lhsT=w2c.bitcast(FP8X4), lhsT_scale=w2s,
                     rhs=codes.bitcast(FP8X4), rhs_scale=scales, start=True, stop=True)
-            copy = nc.vector.tensor_copy if grp[-1] == LAST else nc.scalar.copy
+            copy = nc.vector.tensor_copy if grp == W2_LOADS[-3] else nc.scalar.copy
             copy(out=y_sb[:, grp[0] * C:(grp[-1] + 1) * C], in_=acc[:, 0:len(grp), :].rearrange("p e c -> p (e c)"))
 
         def shared(u, e):
@@ -219,7 +219,7 @@ def tile_routed_moe_kernel(tc, xT, w1, w3, w2, gate, offs, pos1, pos2, out):
         round_w2(7, 1)
         quant_w2(6, 1)
         quant_w2(7, 1)
-        y_sb = held.tile([P, SLOTS], F32, name="y_sb", tag=f"w2_raw{W2_LOADS[-3][0]}", align_bytes=DMA_ALIGN)
+        y_sb = held.tile([P, SLOTS], F32, name="y_sb", tag=f"w2_raw{LAST}", align_bytes=DMA_ALIGN)
         for grp in W2_LOADS:
             second_layer(grp)
 

@@ -92,12 +92,12 @@ def tile_routed_moe_kernel(tc, xT, w1, w3, w2, gate, offs, pos1, pos2, out):
         def round_w(u, e, on_vector, on_scalar):
             if u == 0:
                 live["g", e] = stage.tile([P, 2, H * J], BF16, name="grouped", align_bytes=64)
-            src = w_raw[u, e].rearrange("p (j m t) -> p m j t", j=J, t=4)
-            dst = live["g", e][:, u, :].rearrange("p (t m j) -> p m j t", t=4, j=J)
+            src = w_raw[u, e].rearrange("p (j m s t) -> p s m j t", j=J, s=2, t=2)
+            dst = live["g", e][:, u, :].rearrange("p (s t m j) -> p s m j t", s=2, t=2, j=J)
             for part in on_vector:
-                nc.vector.tensor_copy(out=dst[:, part], in_=src[:, part])
+                nc.vector.tensor_copy(out=dst[:, :, part], in_=src[:, :, part])
             for part in on_scalar:
-                nc.scalar.copy(out=dst[:, part], in_=src[:, part])
+                nc.scalar.copy(out=dst[:, :, part], in_=src[:, :, part])
 
         def first_layer(us, e):
             n = len(us)
@@ -147,9 +147,9 @@ def tile_routed_moe_kernel(tc, xT, w1, w3, w2, gate, offs, pos1, pos2, out):
 
         def round_w2(first, count):
             g = load_of[first]
-            src = w2_raw[g][:, first - g[0]:first - g[0] + count].rearrange("p e (j c i) -> p e c j i", j=J, i=4)
+            src = w2_raw[g][:, first - g[0]:first - g[0] + count].rearrange("p e (j c i) -> p e c j i", j=J, i=2)
             staged = {1: early[:, 0:4 * C].unsqueeze(1), 5: late[:, 0:1]}.get(first, w2_staged[:, first:first + count])
-            dst = staged.rearrange("p e (c i j) -> p e c j i", i=4, j=J)
+            dst = staged.rearrange("p e (c i j) -> p e c j i", i=2, j=J)
             copy = nc.vector.tensor_copy if first in W2_ON_VECTOR else nc.scalar.copy
             if count == 1:
                 copy(out=dst[:, 0], in_=src[:, 0])

from contextlib import ExitStack

import concourse.mybir as mybir

K, T, E, C, H, N = 512, 512, 8, 128, 512, 128
SLOTS = E * C
FLOPS = 2 * SLOTS * (2 * K * H + H * N)

F32 = mybir.dt.float32
BF16 = mybir.dt.bfloat16
U32 = mybir.dt.uint32
U16 = mybir.dt.uint16
U8 = mybir.dt.uint8
FP8X4 = mybir.dt.float8_e4m3fn_x4
MULT = mybir.AluOpType.mult
ADD = mybir.AluOpType.add
SILU = mybir.ActivationFunctionType.Silu
COPY = mybir.ActivationFunctionType.Copy

P = 128
J = 4
DMA_ALIGN = 256
LAST = E - 1
W2_LOADS = ((0, 1), (2, 3), (4, 5), (6,), (7,))
W2_ON_VECTOR = (1, 5, 7)
ROW = J * H
LAP = 32
PIECE = C * 4 // 2
FIRST_PART = 256
GATHERS = {0: (0, 2), 1: (2, 3), 2: (5, 3)}
X_ON_VECTOR = 344
ON_SCALAR = {(0, E - 2): 104, (1, E - 2): 48, (0, E - 1): 76, (1, E - 1): 50}


def tile_routed_moe_kernel(tc, xT, w1, w3, w2, gate, offs, pos1, pos2, out):
    nc = tc.nc
    with ExitStack() as ctx:
        held = ctx.enter_context(tc.tile_pool(name="held", bufs=1))
        stage = ctx.enter_context(tc.tile_pool(name="stage", bufs=2))
        psum = ctx.enter_context(tc.psum_pool(name="psum", bufs=1))

        offs_t = held.tile([P, SLOTS // 16], U16, name="offs_t")
        pos1_t = held.tile([P, T // 16], U16, name="pos1_t")
        pos2_t = held.tile([P, T // 16], U16, name="pos2_t")
        x_raw = held.tile([P, J, T], F32, name="x_raw", align_bytes=DMA_ALIGN)
        gates = held.tile([P, 2, T], F32, name="gates", align_bytes=DMA_ALIGN)
        ahead = {(1, LAST): 2 * PIECE}
        behind = {(1, LAST): 2 * PIECE}
        w_tile = {(u, e): held.tile([P, ahead.get((u, e), 0) + ROW + behind.get((u, e), 0)], F32, name=f"w_raw{u}_{e}", align_bytes=DMA_ALIGN)
                  for e in range(E) for u in range(2)}
        w_raw = {k: t[:, ahead.get(k, 0):ahead.get(k, 0) + ROW] for k, t in w_tile.items()}
        w2_raw = {g: held.tile([P, len(g), J * N], F32, name=f"w2_raw{g[0]}", align_bytes=DMA_ALIGN) for g in W2_LOADS}

        nc.sync.dma_start(out=x_raw[:], in_=xT.rearrange("(p j) t -> p j t", j=J))
        nc.sync.dma_start(offs_t[:], offs)
        for e in range(E):
            for u, w in enumerate((w1, w3)):
                nc.sync.dma_start(out=w_raw[u, e], in_=w[e, :, :].rearrange("(p j) h -> p (j h)", j=J))
        for g in W2_LOADS:
            nc.sync.dma_start(out=w2_raw[g][:], in_=w2[g[0]:g[-1] + 1, :, :].rearrange("e (p j) n -> p e (j n)", j=J))
        for lst, pos, g in ((pos1_t, pos1, 0), (pos2_t, pos2, 1)):
            nc.sync.dma_start(lst[:], pos)
            nc.sync.dma_start(out=gates[:, g, :], in_=gate[g, :, :])

        x_codes = held.tile([P, T], U32, name="x_codes", align_bytes=64)
        x_scales = held.tile([P, T], U8, name="x_scales", align_bytes=64)
        nc.gpsimd.memset(x_scales[:], 0)
        x_grouped = held.tile([P, T * J], BF16, name="x_grouped", align_bytes=64)
        x_src = x_raw[:].rearrange("p j (c i) -> p c j i", i=4)
        x_dst = x_grouped[:].rearrange("p (c i j) -> p c j i", i=4, j=J)
        cut = X_ON_VECTOR // 4
        nc.vector.tensor_copy(out=x_dst[:, 0:cut], in_=x_src[:, 0:cut])
        nc.scalar.copy(out=x_dst[:, cut:], in_=x_src[:, cut:])
        nc.vector.quantize_mx(out=x_codes[:].bitcast(FP8X4), scales=x_scales[:], in_=x_grouped[:])

        s_codes = held.tile([P, SLOTS], U32, name="s_codes", align_bytes=64)
        s_scales = held.tile([P, SLOTS], U8, name="s_scales", align_bytes=64)
        h_early = held.tile([P, LAST - 2, C * 4], BF16, name="h_early", align_bytes=64)
        early = w_tile[1, LAST][:, 0:3 * PIECE].bitcast(BF16)
        late = held.tile([P, 2, C * 4], BF16, name="late", align_bytes=64)
        h_of = {e: h_early[:, e, :] for e in range(LAST - 2)}
        h_of[LAST - 2], h_of[LAST - 1], h_of[LAST] = early[:, 4 * C:8 * C], early[:, 8 * C:], late[:, 1, :]
        sil_behind = {LAST: (1, LAST)}
        live = {}

        def gather(first, count):
            cols = slice(first * C, (first + count) * C)
            lst = offs_t[:, first * C // 16:(first + count) * C // 16]
            nc.vector.tensor_copy(s_codes[:, cols], x_codes[:].indirect(lst))
            nc.vector.tensor_copy(s_scales[:, cols], x_scales[:].indirect(lst))

        def round_w(u, e, on_vector, on_scalar):
            if u == 0:
                live["g", e] = stage.tile([P, 2, H * J], BF16, name="grouped", align_bytes=64)
            src = w_raw[u, e].rearrange("p (j m s t) -> p s m j t", j=J, s=2, t=2)
            dst = live["g", e][:, u, :].rearrange("p (s t m j) -> p s m j t", s=2, t=2, j=J)
            for part in on_vector:
                nc.vector.tensor_copy(out=dst[:, :, part], in_=src[:, :, part])
            for part in on_scalar:
                nc.scalar.copy(out=dst[:, :, part], in_=src[:, :, part])

        def first_layer(us, e):
            n = len(us)
            codes = stage.tile([P, n * H], U32, name=f"codes{n}", align_bytes=64)
            scales = stage.tile([P, n * H], U8, name=f"scales{n}", align_bytes=64)
            nc.vector.quantize_mx(out=codes[:].bitcast(FP8X4), scales=scales[:],
                                  in_=live["g", e][:, us[0]:us[-1] + 1, :].rearrange("p u k -> p (u k)"))
            cols = slice(e * C, (e + 1) * C)
            order = list(enumerate(us))
            for i, u in order if e == LAST - 1 else reversed(order):
                acc = psum.tile([P, 4, C], F32, name=f"acc{u}", bufs=2)
                for t in range(4):
                    blk = slice(i * H + t * P, i * H + (t + 1) * P)
                    nc.tensor.matmul_mx(
                        out=acc[:, t, :], lhsT=codes[:, blk].bitcast(FP8X4), lhsT_scale=scales[:, blk],
                        rhs=s_codes[:, cols].bitcast(FP8X4), rhs_scale=s_scales[:, cols], start=True, stop=True)
                live["acc", u, e] = acc

        def silu(e):
            if e in sil_behind:
                start = ahead.get(sil_behind[e], 0) + ROW - LAP
                sil = w_tile[sil_behind[e]][:, start:start + 4 * C].rearrange("p (c t) -> p c t", t=4)
            else:
                tag = f"w_raw1_{e + 1}" if e < LAST - 1 else f"w_raw0_{LAST}"
                own = held.tile([P, C, 4], F32, name=f"sil{e}", tag=tag, align_bytes=DMA_ALIGN)
                sil = own[:]
            nc.scalar.activation(sil, live["acc", 0, e][:].rearrange("p t c -> p c t"), SILU)
            live["sil", e] = sil

        def hidden(e):
            nc.vector.tensor_tensor(h_of[e].rearrange("p (c t) -> p c t", t=4), live["acc", 1, e][:].rearrange("p t c -> p c t"), live["sil", e], MULT)

        def quant_pieces(names, values):
            n = len(names)
            codes = held.tile([P, n, C], U32, name=f"codes_{names[0][0]}{names[0][1]}", align_bytes=64)
            scales = held.tile([P, n, C], U8, name=f"scales_{names[0][0]}{names[0][1]}", align_bytes=64)
            nc.vector.quantize_mx(out=codes[:].rearrange("p e c -> p (e c)").bitcast(FP8X4),
                                  scales=scales[:].rearrange("p e c -> p (e c)"), in_=values)
            for i, name in enumerate(names):
                live[name] = codes[:, i, :], scales[:, i, :]

        def quant_h_early(group):
            quant_pieces([("qh", i) for i in group], h_early[:, group.start:group.stop].rearrange("p e n -> p (e n)"))

        w2_staged = held.tile([P, E, N * J], BF16, name="w2_staged", tag="w_raw0_3", align_bytes=DMA_ALIGN)
        load_of = {e: g for g in W2_LOADS for e in g}

        def round_w2(first, count):
            g = load_of[first]
            src = w2_raw[g][:, first - g[0]:first - g[0] + count].rearrange("p e (j c i) -> p e c j i", j=J, i=2)
            staged = {1: early[:, 0:4 * C].unsqueeze(1), 5: late[:, 0:1]}.get(first, w2_staged[:, first:first + count])
            dst = staged.rearrange("p e (c i j) -> p e c j i", i=2, j=J)
            copy = nc.vector.tensor_copy if first in W2_ON_VECTOR else nc.scalar.copy
            if count == 1:
                copy(out=dst[:, 0], in_=src[:, 0])
            else:
                copy(out=dst, in_=src)

        def quant_w2(first, count):
            quant_pieces([("w2", e) for e in range(first, first + count)],
                         w2_staged[:, first:first + count].rearrange("p e n -> p (e n)"))

        def second_layer(grp):
            if grp[0] == 0:
                acc = psum.tile([P, 4, C], F32, name="acc_y0", tag="acc0", bufs=2)
            else:
                acc = psum.tile([P, 4, C], F32, name=f"acc_y{grp[0]}")
            for i, e in enumerate(grp):
                codes, scales = live["qh", e]
                w2c, w2s = live["w2", e]
                nc.tensor.matmul_mx(
                    out=acc[:, i, :], lhsT=w2c.bitcast(FP8X4), lhsT_scale=w2s,
                    rhs=codes.bitcast(FP8X4), rhs_scale=scales, start=True, stop=True)
            copy = nc.vector.tensor_copy if grp == W2_LOADS[-3] else nc.scalar.copy
            copy(out=y_sb[:, grp[0] * C:(grp[-1] + 1) * C], in_=acc[:, 0:len(grp), :].rearrange("p e c -> p (e c)"))

        def shared(u, e):
            n = ON_SCALAR[u, e]
            on_scalar, on_vector = (slice(0, n), slice(n, P)) if (u, e) == (1, LAST) else (slice(P - n, P), slice(0, P - n))
            round_w(u, e, [on_vector], [on_scalar])

        for e in range(LAST):
            if e in GATHERS:
                gather(*GATHERS[e])
            if (0, e) in ON_SCALAR:
                shared(0, e)
                quant_h_early(range(e - 3, e - 1))
            else:
                round_w(0, e, [], [slice(0, P)])
            if (1, e) in ON_SCALAR:
                shared(1, e)
            else:
                round_w(1, e, [slice(0, P)], [])
            first_layer((0, 1), e)
            if e:
                silu(e - 1)
                hidden(e - 1)
            if e in (1, 3):
                quant_h_early(range(max(e - 2, 0), e))
        shared(0, LAST)
        first_layer((0,), LAST)
        silu(LAST - 1)
        shared(1, LAST)
        first_layer((1,), LAST)
        silu(LAST)
        round_w2(0, 1)
        round_w2(1, 1)
        hidden(LAST - 1)
        quant_w2(0, 1)
        quant_pieces([("w2", 1), ("qh", LAST - 2), ("qh", LAST - 1)], early)
        hidden(LAST)
        round_w2(2, 2)
        round_w2(4, 1)
        round_w2(5, 1)
        quant_w2(2, 2)
        quant_pieces([("w2", 5), ("qh", LAST)], late[:].rearrange("p e n -> p (e n)"))
        quant_w2(4, 1)
        round_w2(6, 1)
        round_w2(7, 1)
        quant_w2(6, 1)
        quant_w2(7, 1)
        y_sb = held.tile([P, SLOTS], F32, name="y_sb", tag=f"w2_raw{LAST}", align_bytes=DMA_ALIGN)
        for grp in W2_LOADS:
            second_layer(grp)

        r1 = held.tile([P, T], F32, name="r1", tag="x_raw", align_bytes=DMA_ALIGN)
        r2 = held.tile([P, T], F32, name="r2", tag="w_raw0_0", align_bytes=DMA_ALIGN)
        res = held.tile([P, T], F32, name="res", tag="w_raw0_1", align_bytes=DMA_ALIGN)
        p2 = held.tile([P, T], F32, name="p2", tag="w_raw0_2", align_bytes=DMA_ALIGN)
        parts = slice(0, FIRST_PART), slice(FIRST_PART, T)
        nc.vector.tensor_tensor(r1[:], y_sb[:].indirect(pos1_t[:]), gates[:, 0, :], MULT)
        for toks in parts:
            nc.scalar.activation(r2[:, toks], y_sb[:].indirect(pos2_t[:, toks.start // 16:toks.stop // 16]), COPY)
        for toks in parts:
            nc.vector.tensor_tensor(p2[:, toks], r2[:, toks], gates[:, 1, toks], MULT)
        for toks in parts:
            nc.vector.tensor_tensor(res[:, toks], r1[:, toks], p2[:, toks], ADD)
            nc.scalar.dma_start(out=out[:, toks], in_=res[:, toks])
